import numpy as np
import ml_dtypes


def mxq(x, axis, fmt="e4m3"):
    dtype, down = {"e4m3": (ml_dtypes.float8_e4m3fn, 7), "e5m2": (ml_dtypes.float8_e5m2, 14)}[fmt]
    v = np.moveaxis(np.asarray(x, np.float32).astype(ml_dtypes.bfloat16).astype(np.float64), axis, -1)
    blocks = v.reshape(v.shape[:-1] + (-1, 32))
    amax = np.abs(blocks).max(-1, keepdims=True)
    byte = np.maximum(np.where(amax > 0, np.frexp(amax)[1] - 1 + 127, 0) - down, 1)
    scale = np.exp2(byte - 127.0)
    codes = (blocks / scale).astype(np.float32).astype(dtype).astype(np.float64)
    return np.moveaxis((codes * scale).reshape(v.shape), -1, axis)


WIDE = False


def mx_kscale(k):
    if not WIDE:
        return np.ones(k)
    levels = np.array([10, -10, 5, -5, 0])
    if k % 512:
        return np.exp2(np.random.permutation(np.resize(levels, k // 32))).repeat(32)
    a = np.empty((k // 512, 16))
    for p in range(k // 512):
        a[p, :8] = np.random.permutation(np.resize(levels, 8))
        for g in range(8):
            far = levels[np.abs(levels - a[p, g]) >= 10]
            a[p, g + 8] = far[np.random.randint(len(far))]
    return np.exp2(a.ravel()).repeat(32)


BF16 = ml_dtypes.bfloat16


def bf(x):
    return np.asarray(x, np.float32).astype(BF16)


def f64(x):
    return np.asarray(x).astype(np.float64)


B, H, T, S, E = 2, 2, 2048, 512, 512


def draw0():
    t = mx_kscale(S)
    return {"q": bf(np.random.standard_normal((B, H, T, E))),
            "k": bf(np.random.standard_normal((B, H, S, E))),
            "v": bf(np.random.standard_normal((B, H, S, E)) / t[:, None]),
            "mixl": bf(np.random.standard_normal((H, H)) / np.sqrt(H)),
            "mixw": bf(np.random.standard_normal((H, H)) / np.sqrt(H)),
            "gs": bf((1.0 + 0.1 * np.random.standard_normal(S)) * t)}


def mix_heads(x, w):
    return np.sum(w[None, :, :, None, None] * x[:, :, None, :, :], axis=1)


def core(q, k, v, mixl, mixw, gs):
    l = f64(q) @ f64(k).transpose(0, 1, 3, 2) / np.sqrt(E)
    m = mix_heads(l, f64(mixl))
    e = np.exp(m - m.max(-1, keepdims=True))
    p = e / e.sum(-1, keepdims=True)
    c = mix_heads(p, f64(mixw))
    u = np.sqrt(S) * c * f64(gs)[None, None, None, :]
    return mxq(u, 3, "e4m3") @ mxq(f64(v), 2, "e4m3")


def e4m3fn_bytes(y):
    return np.clip(np.asarray(y, np.float64), -448.0, 448.0).astype(np.float32).astype(ml_dtypes.float8_e4m3fn).view(np.uint8)


def e4m3fn_values(b):
    return np.asarray(b, np.uint8).view(ml_dtypes.float8_e4m3fn).astype(np.float64)


def setup_inputs():
    d = draw0()
    x0 = np.asarray(d['v']).astype(np.float64)
    s = (np.max(np.abs(x0), axis=(0, 1, 3), keepdims=True) / 448.0).astype(np.float32)
    out = {}
    for k, v in d.items():
        if k == 'v':
            out['v_bytes'] = e4m3fn_bytes(x0 / s.astype(np.float64))
            out['v_scale'] = s
        else:
            out[k] = v
    return out


def reference(q, k, v_bytes, v_scale, mixl, mixw, gs):
    return core(q, k, e4m3fn_values(v_bytes) * v_scale.astype(np.float64), mixl, mixw, gs)

@@ -1,0 +1,351 @@
+import math
+from contextlib import ExitStack
+
+import concourse.mybir as mybir
+from concourse.masks import make_identity
+
+B, H, T, S, E = 2, 2, 2048, 512, 512
+FLOPS = 2 * 2 * B * H * T * S * E
+
+F32 = mybir.dt.float32
+BF16 = mybir.dt.bfloat16
+U32 = mybir.dt.uint32
+U8 = mybir.dt.uint8
+FP8 = mybir.dt.float8_e4m3fn
+FP8X4 = mybir.dt.float8_e4m3fn_x4
+ALU = mybir.AluOpType
+ACT = mybir.ActivationFunctionType
+AXIS = mybir.AxisListType
+
+P = 128
+PACK = 4
+TILES_PER_BATCH = T // P
+N_TILES = B * TILES_PER_BATCH
+
+
+def tile_caittalkingheadsattention_t_kernel(tc, q, k, v_bytes, v_scale, mixl, mixw, gs, out):
+    nc = tc.nc
+    with ExitStack() as ctx:
+        keep = ctx.enter_context(tc.tile_pool(name="keep", bufs=1))
+        ring2 = ctx.enter_context(tc.tile_pool(name="ring2", bufs=2))
+        ring3 = ctx.enter_context(tc.tile_pool(name="ring3", bufs=3))
+        ring4 = ctx.enter_context(tc.tile_pool(name="ring4", bufs=4))
+        psum = ctx.enter_context(tc.psum_pool(name="psum", bufs=1))
+        ctx.enter_context(tc.manual_schedule())
+
+        q_rows, q_bank, q_turned, scaled, logits, neg_max, expo, sums = {}, {}, {}, {}, {}, {}, {}, {}
+        shares, u_wide, u_codes, u_scales, mix_bank, out_bank, l_bank = {}, {}, {}, {}, {}, {}, {}
+        k_rows, k_turned, v_raw, v_wide, v_woven, v_codes, v_scales = {}, {}, {}, {}, {}, {}, {}
+
+        def live(n):
+            return 0 <= n < N_TILES
+
+        def token_rows(dram, n):
+            b, i = divmod(n, TILES_PER_BATCH)
+            return dram[b, :, i * P : (i + 1) * P, :].rearrange("h p e -> p h e")
+
+        def load_q(n):
+            q_rows[n] = ring4.tile([P, H, E], BF16, name="q_rows")
+            nc.sync.dma_start(out=q_rows[n][:], in_=token_rows(q, n))
+
+        def load_k(b, h):
+            k_rows[b, h] = keep.tile([P, PACK, E], BF16, name="k_rows_%d%d" % (b, h))
+            nc.sync.dma_start(out=k_rows[b, h][:], in_=k[b, h].rearrange("(p t) e -> p t e", t=PACK))
+
+        def load_v(b):
+            v_raw[b] = keep.tile([P, H, PACK * E], U8, name="v_raw_%d" % b)
+            nc.sync.dma_start(out=v_raw[b][:], in_=v_bytes[b].rearrange("h (p t) e -> p h (t e)", t=PACK))
+
+        mixl_raw = keep.tile([P, H * H], BF16, name="mixl_raw")
+        mixw_raw = keep.tile([P, H * H], BF16, name="mixw_raw")
+        gs_raw = keep.tile([P, PACK], BF16, name="gs_raw")
+        v_row_scale = keep.tile([P, PACK], F32, name="v_row_scale")
+
+        load_k(0, 1)
+        load_q(0)
+        nc.sync.dma_start(out=mixl_raw[:], in_=mixl.rearrange("h j -> (h j)").partition_broadcast(P))
+        nc.sync.dma_start(out=v_row_scale[:], in_=v_scale.rearrange("a b (p t) c -> p (a b t c)", t=PACK))
+        load_v(0)
+        load_k(0, 0)
+        load_q(1)
+        load_q(2)
+        load_v(1)
+        load_k(1, 1)
+        load_k(1, 0)
+        nc.sync.dma_start(out=mixw_raw[:], in_=mixw.rearrange("h j -> (h j)").partition_broadcast(P))
+        nc.sync.dma_start(out=gs_raw[:], in_=gs.rearrange("(p t) -> p t", t=PACK))
+        load_q(3)
+
+        ident_bf16 = keep.tile([P, P], BF16, name="ident_bf16")
+        ident_f32 = keep.tile([P, P], F32, name="ident_f32")
+        make_identity(nc, ident_bf16[:])
+        make_identity(nc, ident_f32[:])
+
+        warm_in = keep.tile([P, 1], F32, name="warm_in")
+        warm_out = keep.tile([P, 1], F32, name="warm_out")
+        nc.vector.memset(warm_in[:], 0.0)
+        nc.scalar.activation(out=warm_out[:], in_=warm_in[:], func=ACT.Exp)
+
+        logit_mix = keep.tile([P, H * H], F32, name="logit_mix")
+        weight_mix = keep.tile([P, H * H], F32, name="weight_mix")
+        key_gain = keep.tile([P, P, PACK], F32, name="key_gain")
+
+        def turn_k_steps(b, h, banks):
+            steps = []
+            for c in range(PACK):
+                half, parity = divmod(c, 2)
+                e0 = 256 * half + parity
+                for t in range(PACK):
+                    steps.append((turn_k, (b, h, c, t, e0, banks[c % len(banks)])))
+            return steps
+
+        k_bank = {}
+
+        def turn_k(b, h, c, t, e0, bank):
+            if t == 0:
+                k_bank[b, h, c] = psum.tile([P, S], BF16, name="k_bank", tag=bank)
+            nc.tensor.transpose(
+                k_bank[b, h, c][:, t * P : (t + 1) * P], k_rows[b, h][:, t, e0 : e0 + 255 : 2], ident_bf16[:]
+            )
+            if t == PACK - 1:
+                k_turned[b, h, c] = keep.tile([P, S], BF16, name="k_turned_%d%d%d" % (b, h, c))
+                nc.vector.tensor_copy(out=k_turned[b, h, c][:], in_=k_bank[b, h, c][:])
+
+        def turn_q(n, c):
+            if c == 0:
+                q_bank[n] = psum.tile([P, PACK, P], F32, name="q_bank", tag="q")
+            words = q_rows[n][:].rearrange("p h e -> p (h e)").bitcast(F32)
+            nc.tensor.transpose(q_bank[n][:, c, :], words[:, c * P : (c + 1) * P], ident_f32[:])
+
+        def copy_q(n):
+            q_turned[n] = ring2.tile([P, PACK * P], F32, name="q_turned")
+            nc.scalar.copy(out=q_turned[n][:], in_=q_bank[n][:].rearrange("p c n -> p (c n)"))
+
+        def logit_pass(n, h, c):
+            if c == 0:
+                l_bank[n, h] = psum.tile([P, S], F32, name="l_bank", tag="l%d" % h)
+            half, parity = divmod(c, 2)
+            col0 = (2 * h + half) * 2 * P + parity
+            pairs = q_turned[n][:].bitcast(BF16)
+            nc.tensor.matmul(
+                l_bank[n, h][:],
+                lhsT=pairs[:, col0 : col0 + 2 * P - 1 : 2],
+                rhs=k_turned[n // TILES_PER_BATCH, h, c][:],
+                start=(c == 0),
+                stop=(c == PACK - 1),
+            )
+
+        def scale_head1(n):
+            scaled[n] = ring2.tile([P, H, S], F32, name="scaled")
+            for j in range(H):
+                nc.scalar.activation(
+                    out=scaled[n][:, j, :], in_=l_bank[n, 1][:], func=ACT.Copy, scale=logit_mix[:, H + j : H + j + 1]
+                )
+
+        def mix_logits(n):
+            logits[n] = ring2.tile([P, H, S], F32, name="logits")
+            for j in range(H):
+                nc.vector.scalar_tensor_tensor(
+                    out=logits[n][:, j, :],
+                    in0=l_bank[n, 0][:],
+                    scalar=logit_mix[:, j : j + 1],
+                    in1=scaled[n][:, j, :],
+                    op0=ALU.mult,
+                    op1=ALU.add,
+                )
+
+        def row_max(n):
+            neg_max[n] = ring3.tile([P, H], F32, name="neg_max")
+            nc.vector.tensor_reduce(out=neg_max[n][:], in_=logits[n][:], axis=AXIS.X, op=ALU.max, negate=True)
+
+        def exponentials(n):
+            expo[n] = ring2.tile([P, H, S], F32, name="expo")
+            sums[n] = ring3.tile([P, H], F32, name="sums")
+            for h in range(H):
+                nc.scalar.activation(
+                    out=expo[n][:, h, :],
+                    in_=logits[n][:, h, :],
+                    func=ACT.Exp,
+                    bias=neg_max[n][:, h : h + 1],
+                    accum_out=sums[n][:, h : h + 1],
+                )
+
+        def weigh_heads(n, engine):
+            inv_sum = ring3.tile([P, H], F32, name="inv_sum")
+            nc.vector.reciprocal(out=inv_sum[:], in_=sums[n][:])
+            for j in range(H):
+                for h in range(H):
+                    shares[n, j, h] = ring2.tile([P, S], F32, name="share_%d%d" % (j, h))
+                    engine.tensor_scalar(
+                        out=shares[n, j, h][:],
+                        in0=expo[n][:, h, :],
+                        scalar1=inv_sum[:, h : h + 1],
+                        scalar2=weight_mix[:, H * h + j : H * h + j + 1],
+                        op0=ALU.mult,
+                        op1=ALU.mult,
+                    )
+
+        def turn_share(n, j, t, h):
+            if t == 0 and h == 0:
+                mix_bank[n, j] = psum.tile([P, PACK, P], F32, name="mix_bank", tag="m%d" % j)
+            nc.tensor.matmul(
+                mix_bank[n, j][:, t, :],
+                lhsT=shares[n, j, h][:, t * P : (t + 1) * P],
+                rhs=ident_f32[:],
+                is_transpose=True,
+                start=(h == 0),
+                stop=(h == H - 1),
+            )
+
+        def apply_gain(n, j):
+            if j == 0:
+                u_wide[n] = ring2.tile([P, H, P, PACK], BF16, name="u_wide", align_bytes=64)
+            nc.vector.tensor_tensor(
+                out=u_wide[n][:, j, :, :],
+                in0=mix_bank[n, j][:].rearrange("p t n -> p n t"),
+                in1=key_gain[:],
+                op=ALU.mult,
+            )
+
+        def quantise_u(n):
+            u_codes[n] = ring2.tile([P, H * P], U32, name="u_codes", align_bytes=64)
+            u_scales[n] = ring2.tile([P, H * P], U8, name="u_scales", align_bytes=64)
+            nc.vector.quantize_mx(
+                out=u_codes[n][:].bitcast(FP8X4),
+                scales=u_scales[n][:],
+                in_=u_wide[n][:].rearrange("p j n t -> p (j n t)"),
+            )
+
+        def mix_values(n):
+            b = n // TILES_PER_BATCH
+            for j in range(H):
+                out_bank[n, j] = psum.tile([P, E], F32, name="out_bank", tag="o%d" % j)
+                nc.tensor.matmul_mx(
+                    out=out_bank[n, j][:],
+                    lhsT=u_codes[n][:, j * P : (j + 1) * P].bitcast(FP8X4),
+                    lhsT_scale=u_scales[n][:, j * P : (j + 1) * P],
+                    rhs=v_codes[b, j][:].bitcast(FP8X4),
+                    rhs_scale=v_scales[b, j][:],
+                    start=True,
+                    stop=True,
+                )
+
+        def store(n):
+            result = ring3.tile([P, H, E], F32, name="result")
+            for j in range(H):
+                nc.scalar.copy(out=result[:, j, :], in_=out_bank[n, j][:])
+            nc.sync.dma_start(out=token_rows(out, n), in_=result[:])
+
+        def widen_v(b, j):
+            v_wide[b, j] = ring2.tile([P, PACK, E], BF16, name="v_wide")
+            for t in range(PACK):
+                nc.scalar.activation(
+                    out=v_wide[b, j][:, t, :],
+                    in_=v_raw[b][:, j, t * E : (t + 1) * E].bitcast(FP8),
+                    func=ACT.Copy,
+                    scale=v_row_scale[:, t : t + 1],
+                )
+
+        def weave_v(b, j):
+            v_woven[b, j] = ring2.tile([P, E, PACK], BF16, name="v_woven", align_bytes=64)
+            planes = v_wide[b, j][:].rearrange("p t e -> p e t")
+            if b == 0:
+                nc.gpsimd.tensor_scalar(
+                    out=v_woven[b, j][:], in0=planes, scalar1=1.0, scalar2=0.0, op0=ALU.mult, op1=ALU.add
+                )
+            else:
+                nc.vector.tensor_copy(out=v_woven[b, j][:], in_=planes)
+
+        def quantise_v(b, j):
+            v_codes[b, j] = keep.tile([P, E], U32, name="v_codes_%d%d" % (b, j), align_bytes=64)
+            v_scales[b, j] = keep.tile([P, E], U8, name="v_scales_%d%d" % (b, j), align_bytes=64)
+            nc.vector.quantize_mx(
+                out=v_codes[b, j][:].bitcast(FP8X4),
+                scales=v_scales[b, j][:],
+                in_=v_woven[b, j][:].rearrange("p e t -> p (e t)"),
+            )
+
+        def run(steps):
+            for fn, args in steps:
+                fn(*args)
+
+        def passes_with_gaps(n, h, gaps):
+            for c in range(PACK):
+                if live(n):
+                    logit_pass(n, h, c)
+                run(gaps[c])
+
+        def deal(steps, n_gaps):
+            per_gap = -(-len(steps) // n_gaps)
+            gaps = [steps[g * per_gap : (g + 1) * per_gap] for g in range(n_gaps)]
+            return gaps + [[] for g in range(PACK - n_gaps)]
+
+        run(turn_k_steps(0, 1, ["m0", "m1", "o0", "o1"]))
+        nc.vector.tensor_scalar(
+            out=logit_mix[:], in0=mixl_raw[:], scalar1=1.0 / math.sqrt(E), scalar2=None, op0=ALU.mult
+        )
+        k_jobs = {0: (0, 0), 1: (1, 1), 2: (1, 0)}
+        widen_jobs = {-1: (0, 0), 0: (0, 1), 1: (1, 0), 2: (1, 1)}
+
+        for n in range(-2, N_TILES + 4):
+            if n >= 0 and live(n + 4):
+                load_q(n + 4)
+            if live(n - 1):
+                row_max(n - 1)
+            if live(n + 1):
+                copy_q(n + 1)
+            if live(n - 4):
+                quantise_u(n - 4)
+            if n == 1:
+                nc.vector.tensor_copy(out=weight_mix[:], in_=mixw_raw[:])
+                nc.vector.tensor_scalar(
+                    out=key_gain[:],
+                    in0=gs_raw[:].rearrange("p (o t) -> p o t", o=1).to_broadcast([P, P, PACK]),
+                    scalar1=math.sqrt(S),
+                    scalar2=None,
+                    op0=ALU.mult,
+                )
+            if n == 2:
+                quantise_v(0, 0)
+                quantise_v(0, 1)
+                weave_v(1, 0)
+            if n == 3:
+                quantise_v(1, 0)
+                weave_v(1, 1)
+            if n == 4:
+                quantise_v(1, 1)
+            if live(n - 2):
+                weigh_heads(n - 2, nc.vector if n - 2 == N_TILES - 1 else nc.gpsimd)
+
+            first, second = [], []
+            if live(n - 3):
+                first = [(turn_share, (n - 3, 0, t, h)) for t in range(PACK) for h in range(H)]
+                second = [(turn_share, (n - 3, 1, t, h)) for t in range(PACK) for h in range(H)]
+            if n in k_jobs:
+                first = turn_k_steps(k_jobs[n][0], k_jobs[n][1], ["spare", "o0", "o1"])
+            if live(n + 2):
+                second = second + [(turn_q, (n + 2, c)) for c in range(PACK)]
+            n_first = 4 if n in k_jobs else 3
+            gaps_first = deal(first, n_first)
+            gaps_second = deal(second, 4)
+            passes_with_gaps(n, 1, gaps_first)
+            if live(n):
+                scale_head1(n)
+            if live(n - 3):
+                apply_gain(n - 3, 0)
+            run(gaps_second[0])
+            passes_with_gaps(n, 0, gaps_second[1:] + [[]])
+            if live(n - 1):
+                exponentials(n - 1)
+            if live(n):
+                mix_logits(n)
+            if live(n - 4):
+                mix_values(n - 4)
+            if live(n - 3):
+                apply_gain(n - 3, 1)
+            if live(n - 4):
+                store(n - 4)
+            if n in widen_jobs:
+                widen_v(*widen_jobs[n])
+                if widen_jobs[n][0] == 0:
+                    weave_v(*widen_jobs[n])

@@ -21,6 +21,7 @@ P = 128
 PACK = 4
 TILES_PER_BATCH = T // P
 N_TILES = B * TILES_PER_BATCH
+WARM_MATMULS = 6
 
 
 def tile_caittalkingheadsattention_t_kernel(tc, q, k, v_bytes, v_scale, mixl, mixw, gs, out):
@@ -61,20 +62,20 @@ def tile_caittalkingheadsattention_t_kernel(tc, q, k, v_bytes, v_scale, mixl, mi
         gs_raw = keep.tile([P, PACK], BF16, name="gs_raw")
         v_row_scale = keep.tile([P, PACK], F32, name="v_row_scale")
 
-        load_k(0, 1)
         load_q(0)
+        load_k(0, 1)
         nc.sync.dma_start(out=mixl_raw[:], in_=mixl.rearrange("h j -> (h j)").partition_broadcast(P))
         nc.sync.dma_start(out=v_row_scale[:], in_=v_scale.rearrange("a b (p t) c -> p (a b t c)", t=PACK))
         load_v(0)
-        load_k(0, 0)
         load_q(1)
+        load_k(0, 0)
         load_q(2)
         load_v(1)
-        load_k(1, 1)
-        load_k(1, 0)
         nc.sync.dma_start(out=mixw_raw[:], in_=mixw.rearrange("h j -> (h j)").partition_broadcast(P))
         nc.sync.dma_start(out=gs_raw[:], in_=gs.rearrange("(p t) -> p t", t=PACK))
+        load_k(1, 1)
         load_q(3)
+        load_k(1, 0)
 
         ident_bf16 = keep.tile([P, P], BF16, name="ident_bf16")
         ident_f32 = keep.tile([P, P], F32, name="ident_f32")
@@ -90,18 +91,25 @@ def tile_caittalkingheadsattention_t_kernel(tc, q, k, v_bytes, v_scale, mixl, mi
         weight_mix = keep.tile([P, H * H], F32, name="weight_mix")
         key_gain = keep.tile([P, P, PACK], F32, name="key_gain")
 
-        def turn_k_steps(b, h, banks):
+        def turn_k_steps(b, h, engine):
+            banks = ["m0", "m1", "o0", "o1"]
             steps = []
             for c in range(PACK):
                 half, parity = divmod(c, 2)
                 e0 = 256 * half + parity
                 for t in range(PACK):
-                    steps.append((turn_k, (b, h, c, t, e0, banks[c % len(banks)])))
+                    steps.append((turn_k, (b, h, c, t, e0, banks[c], engine)))
             return steps
 
-        k_bank = {}
+        k_bank, inv_sum, factors = {}, {}, {}
 
-        def turn_k(b, h, c, t, e0, bank):
+        def copy(engine, dst, src):
+            if engine is nc.scalar:
+                nc.scalar.copy(out=dst, in_=src)
+            else:
+                engine.tensor_copy(out=dst, in_=src)
+
+        def turn_k(b, h, c, t, e0, bank, engine):
             if t == 0:
                 k_bank[b, h, c] = psum.tile([P, S], BF16, name="k_bank", tag=bank)
             nc.tensor.transpose(
@@ -109,11 +117,11 @@ def tile_caittalkingheadsattention_t_kernel(tc, q, k, v_bytes, v_scale, mixl, mi
             )
             if t == PACK - 1:
                 k_turned[b, h, c] = keep.tile([P, S], BF16, name="k_turned_%d%d%d" % (b, h, c))
-                nc.vector.tensor_copy(out=k_turned[b, h, c][:], in_=k_bank[b, h, c][:])
+                copy(engine, k_turned[b, h, c][:], k_bank[b, h, c][:])
 
         def turn_q(n, c):
             if c == 0:
-                q_bank[n] = psum.tile([P, PACK, P], F32, name="q_bank", tag="q")
+                q_bank[n] = psum.tile([P, PACK, P], F32, name="q_bank", tag="q", bufs=2)
             words = q_rows[n][:].rearrange("p h e -> p (h e)").bitcast(F32)
             nc.tensor.transpose(q_bank[n][:, c, :], words[:, c * P : (c + 1) * P], ident_f32[:])
 
@@ -170,20 +178,43 @@ def tile_caittalkingheadsattention_t_kernel(tc, q, k, v_bytes, v_scale, mixl, mi
                     accum_out=sums[n][:, h : h + 1],
                 )
 
-        def weigh_heads(n, engine):
-            inv_sum = ring3.tile([P, H], F32, name="inv_sum")
-            nc.vector.reciprocal(out=inv_sum[:], in_=sums[n][:])
-            for j in range(H):
-                for h in range(H):
-                    shares[n, j, h] = ring2.tile([P, S], F32, name="share_%d%d" % (j, h))
-                    engine.tensor_scalar(
-                        out=shares[n, j, h][:],
-                        in0=expo[n][:, h, :],
-                        scalar1=inv_sum[:, h : h + 1],
-                        scalar2=weight_mix[:, H * h + j : H * h + j + 1],
-                        op0=ALU.mult,
-                        op1=ALU.mult,
-                    )
+        def invert_sums(n):
+            inv_sum[n] = ring3.tile([P, H], F32, name="inv_sum")
+            nc.vector.reciprocal(out=inv_sum[n][:], in_=sums[n][:])
+
+        def share_factors(n):
+            factors[n] = ring3.tile([P, H, H], F32, name="factors")
+            nc.vector.tensor_tensor(
+                out=factors[n][:],
+                in0=weight_mix[:].rearrange("p (h j) -> p h j", j=H),
+                in1=inv_sum[n][:].rearrange("p (h o) -> p h o", o=1).to_broadcast([P, H, H]),
+                op=ALU.mult,
+            )
+
+        def weigh_head(n, j, h, engine):
+            shares[n, j, h] = ring2.tile([P, S], F32, name="share_%d%d" % (j, h))
+            if engine is nc.vector:
+                nc.vector.tensor_scalar(
+                    out=shares[n, j, h][:],
+                    in0=expo[n][:, h, :],
+                    scalar1=inv_sum[n][:, h : h + 1],
+                    scalar2=weight_mix[:, H * h + j : H * h + j + 1],
+                    op0=ALU.mult,
+                    op1=ALU.mult,
+                )
+            elif engine is nc.scalar:
+                nc.scalar.activation(
+                    out=shares[n, j, h][:], in_=expo[n][:, h, :], func=ACT.Copy, scale=factors[n][:, h, j : j + 1]
+                )
+            else:
+                nc.gpsimd.tensor_scalar(
+                    out=shares[n, j, h][:],
+                    in0=expo[n][:, h, :],
+                    scalar1=factors[n][:, h, j : j + 1],
+                    scalar2=0.0,
+                    op0=ALU.mult,
+                    op1=ALU.add,
+                )
 
         def turn_share(n, j, t, h):
             if t == 0 and h == 0:
@@ -232,24 +263,36 @@ def tile_caittalkingheadsattention_t_kernel(tc, q, k, v_bytes, v_scale, mixl, mi
 
         def store(n):
             result = ring3.tile([P, H, E], F32, name="result")
-            for j in range(H):
-                nc.scalar.copy(out=result[:, j, :], in_=out_bank[n, j][:])
-            nc.sync.dma_start(out=token_rows(out, n), in_=result[:])
+            if n < N_TILES - 1:
+                for j in range(H):
+                    nc.scalar.copy(out=result[:, j, :], in_=out_bank[n, j][:])
+                nc.sync.dma_start(out=token_rows(out, n), in_=result[:])
+            else:
+                for j, engine in enumerate([nc.scalar, nc.vector]):
+                    copy(engine, result[:, j, :], out_bank[n, j][:])
+                    nc.sync.dma_start(out=token_rows(out, n)[:, j, :], in_=result[:, j, :])
 
-        def widen_v(b, j):
+        def widen_v(b, j, engine):
             v_wide[b, j] = ring2.tile([P, PACK, E], BF16, name="v_wide")
             for t in range(PACK):
-                nc.scalar.activation(
-                    out=v_wide[b, j][:, t, :],
-                    in_=v_raw[b][:, j, t * E : (t + 1) * E].bitcast(FP8),
-                    func=ACT.Copy,
-                    scale=v_row_scale[:, t : t + 1],
-                )
+                codes = v_raw[b][:, j, t * E : (t + 1) * E].bitcast(FP8)
+                if engine is nc.scalar:
+                    nc.scalar.activation(
+                        out=v_wide[b, j][:, t, :], in_=codes, func=ACT.Copy, scale=v_row_scale[:, t : t + 1]
+                    )
+                else:
+                    nc.vector.tensor_scalar(
+                        out=v_wide[b, j][:, t, :],
+                        in0=codes,
+                        scalar1=v_row_scale[:, t : t + 1],
+                        scalar2=None,
+                        op0=ALU.mult,
+                    )
 
-        def weave_v(b, j):
+        def weave_v(b, j, engine):
             v_woven[b, j] = ring2.tile([P, E, PACK], BF16, name="v_woven", align_bytes=64)
             planes = v_wide[b, j][:].rearrange("p t e -> p e t")
-            if b == 0:
+            if engine is nc.gpsimd:
                 nc.gpsimd.tensor_scalar(
                     out=v_woven[b, j][:], in0=planes, scalar1=1.0, scalar2=0.0, op0=ALU.mult, op1=ALU.add
                 )
@@ -269,26 +312,41 @@ def tile_caittalkingheadsattention_t_kernel(tc, q, k, v_bytes, v_scale, mixl, mi
             for fn, args in steps:
                 fn(*args)
 
-        def passes_with_gaps(n, h, gaps):
-            for c in range(PACK):
-                if live(n):
-                    logit_pass(n, h, c)
-                run(gaps[c])
+        warm_rows = keep.tile([P, S], BF16, name="warm_rows")
+        nc.vector.memset(warm_rows[:], 0.0)
+        warm_bank = psum.tile([P, S], F32, name="warm_bank", tag="l0")
+        for i in range(WARM_MATMULS):
+            nc.tensor.matmul(warm_bank[:], lhsT=warm_rows[:, :P], rhs=warm_rows[:], start=True, stop=True)
 
-        def deal(steps, n_gaps):
-            per_gap = -(-len(steps) // n_gaps)
-            gaps = [steps[g * per_gap : (g + 1) * per_gap] for g in range(n_gaps)]
-            return gaps + [[] for g in range(PACK - n_gaps)]
-
-        run(turn_k_steps(0, 1, ["m0", "m1", "o0", "o1"]))
+        for c in range(PACK):
+            turn_q(0, c)
+        copy_q(0)
+        first_k = turn_k_steps(0, 1, nc.scalar) + turn_k_steps(0, 0, nc.scalar)
+        run(first_k[: 2 * PACK])
         nc.vector.tensor_scalar(
             out=logit_mix[:], in0=mixl_raw[:], scalar1=1.0 / math.sqrt(E), scalar2=None, op0=ALU.mult
         )
-        k_jobs = {0: (0, 0), 1: (1, 1), 2: (1, 0)}
-        widen_jobs = {-1: (0, 0), 0: (0, 1), 1: (1, 0), 2: (1, 1)}
+        for c in range(PACK):
+            turn_q(1, c)
+        for j in range(H):
+            widen_v(0, j, nc.vector)
+        for j in range(H):
+            weave_v(0, j, nc.vector)
+        for j in range(H):
+            quantise_v(0, j)
+        nc.vector.tensor_copy(out=weight_mix[:], in_=mixw_raw[:])
+        nc.vector.tensor_scalar(
+            out=key_gain[:],
+            in0=gs_raw[:].rearrange("p (o t) -> p o t", o=1).to_broadcast([P, P, PACK]),
+            scalar1=math.sqrt(S),
+            scalar2=None,
+            op0=ALU.mult,
+        )
+        k_jobs = {1: (1, 1, nc.scalar), 2: (1, 0, nc.scalar)}
 
-        for n in range(-2, N_TILES + 4):
-            if n >= 0 and live(n + 4):
+        for n in range(N_TILES + 4):
+            draining = n >= N_TILES
+            if live(n + 4):
                 load_q(n + 4)
             if live(n - 1):
                 row_max(n - 1)
@@ -296,56 +354,60 @@ def tile_caittalkingheadsattention_t_kernel(tc, q, k, v_bytes, v_scale, mixl, mi
                 copy_q(n + 1)
             if live(n - 4):
                 quantise_u(n - 4)
-            if n == 1:
-                nc.vector.tensor_copy(out=weight_mix[:], in_=mixw_raw[:])
-                nc.vector.tensor_scalar(
-                    out=key_gain[:],
-                    in0=gs_raw[:].rearrange("p (o t) -> p o t", o=1).to_broadcast([P, P, PACK]),
-                    scalar1=math.sqrt(S),
-                    scalar2=None,
-                    op0=ALU.mult,
-                )
             if n == 2:
-                quantise_v(0, 0)
-                quantise_v(0, 1)
-                weave_v(1, 0)
+                weave_v(1, 1, nc.vector)
             if n == 3:
-                quantise_v(1, 0)
-                weave_v(1, 1)
-            if n == 4:
                 quantise_v(1, 1)
             if live(n - 2):
-                weigh_heads(n - 2, nc.vector if n - 2 == N_TILES - 1 else nc.gpsimd)
+                weigh_head(n - 2, 0, 0, nc.vector)
+                share_factors(n - 2)
+                if draining:
+                    weigh_head(n - 2, 1, 0, nc.vector)
+                else:
+                    for j, h in [(0, 1), (1, 0), (1, 1)]:
+                        weigh_head(n - 2, j, h, nc.gpsimd)
 
-            first, second = [], []
-            if live(n - 3):
-                first = [(turn_share, (n - 3, 0, t, h)) for t in range(PACK) for h in range(H)]
-                second = [(turn_share, (n - 3, 1, t, h)) for t in range(PACK) for h in range(H)]
-            if n in k_jobs:
-                first = turn_k_steps(k_jobs[n][0], k_jobs[n][1], ["spare", "o0", "o1"])
+            steps = []
             if live(n + 2):
-                second = second + [(turn_q, (n + 2, c)) for c in range(PACK)]
-            n_first = 4 if n in k_jobs else 3
-            gaps_first = deal(first, n_first)
-            gaps_second = deal(second, 4)
-            passes_with_gaps(n, 1, gaps_first)
-            if live(n):
-                scale_head1(n)
+                steps = [(turn_q, (n + 2, c)) for c in range(PACK)]
+            if n == 0:
+                steps = first_k[2 * PACK :] + steps
+            if n in k_jobs:
+                steps = turn_k_steps(*k_jobs[n]) + steps
+            if live(n - 3):
+                steps = steps + [(turn_share, (n - 3, j, t, h)) for j in range(H) for t in range(PACK) for h in range(H)]
+            per_gap = 4 if n == 0 else 3
+            gaps = [steps[g * per_gap : (g + 1) * per_gap] for g in range(2 * PACK)]
+            for c in range(PACK):
+                if live(n):
+                    logit_pass(n, 1, c)
+                    if c == PACK - 1:
+                        scale_head1(n)
+                run(gaps[c])
             if live(n - 3):
                 apply_gain(n - 3, 0)
-            run(gaps_second[0])
-            passes_with_gaps(n, 0, gaps_second[1:] + [[]])
+            for c in range(PACK):
+                if live(n):
+                    logit_pass(n, 0, c)
+                run(gaps[PACK + c])
             if live(n - 1):
                 exponentials(n - 1)
+            if draining and live(n - 2):
+                weigh_head(n - 2, 0, 1, nc.scalar)
+                weigh_head(n - 2, 1, 1, nc.scalar)
             if live(n):
                 mix_logits(n)
             if live(n - 4):
                 mix_values(n - 4)
             if live(n - 3):
                 apply_gain(n - 3, 1)
+            if n == 1:
+                widen_v(1, 1, nc.vector)
+                quantise_v(1, 0)
+            if live(n - 1):
+                invert_sums(n - 1)
             if live(n - 4):
                 store(n - 4)
-            if n in widen_jobs:
-                widen_v(*widen_jobs[n])
-                if widen_jobs[n][0] == 0:
-                    weave_v(*widen_jobs[n])
+            if n == 0:
+                widen_v(1, 0, nc.scalar)
+                weave_v(1, 0, nc.gpsimd)

@@ -22,6 +22,10 @@ PACK = 4
 TILES_PER_BATCH = T // P
 N_TILES = B * TILES_PER_BATCH
 WARM_MATMULS = 6
+MIX_LAG = 4
+OUT_LAG = 5
+PIVOT_SHARE = 2.0**-40
+PIVOT_FLOOR = 2.0**-100
 
 
 def tile_caittalkingheadsattention_t_kernel(tc, q, k, v_bytes, v_scale, mixl, mixw, gs, out):
@@ -62,20 +66,20 @@ def tile_caittalkingheadsattention_t_kernel(tc, q, k, v_bytes, v_scale, mixl, mi
         gs_raw = keep.tile([P, PACK], BF16, name="gs_raw")
         v_row_scale = keep.tile([P, PACK], F32, name="v_row_scale")
 
+        nc.sync.dma_start(out=mixl_raw[:], in_=mixl.rearrange("h j -> (h j)").partition_broadcast(P))
+        nc.sync.dma_start(out=mixw_raw[:], in_=mixw.rearrange("h j -> (h j)").partition_broadcast(P))
         load_q(0)
         load_k(0, 1)
-        nc.sync.dma_start(out=mixl_raw[:], in_=mixl.rearrange("h j -> (h j)").partition_broadcast(P))
+        nc.sync.dma_start(out=gs_raw[:], in_=gs.rearrange("(p t) -> p t", t=PACK))
         nc.sync.dma_start(out=v_row_scale[:], in_=v_scale.rearrange("a b (p t) c -> p (a b t c)", t=PACK))
         load_v(0)
         load_q(1)
         load_k(0, 0)
         load_q(2)
         load_v(1)
-        nc.sync.dma_start(out=mixw_raw[:], in_=mixw.rearrange("h j -> (h j)").partition_broadcast(P))
-        nc.sync.dma_start(out=gs_raw[:], in_=gs.rearrange("(p t) -> p t", t=PACK))
-        load_k(1, 1)
-        load_q(3)
         load_k(1, 0)
+        load_q(3)
+        load_k(1, 1)
 
         ident_bf16 = keep.tile([P, P], BF16, name="ident_bf16")
         ident_f32 = keep.tile([P, P], F32, name="ident_f32")
@@ -87,9 +91,59 @@ def tile_caittalkingheadsattention_t_kernel(tc, q, k, v_bytes, v_scale, mixl, mi
         nc.vector.memset(warm_in[:], 0.0)
         nc.scalar.activation(out=warm_out[:], in_=warm_in[:], func=ACT.Exp)
 
-        logit_mix = keep.tile([P, H * H], F32, name="logit_mix")
-        weight_mix = keep.tile([P, H * H], F32, name="weight_mix")
-        key_gain = keep.tile([P, P, PACK], F32, name="key_gain")
+        def column(name, width=1):
+            return keep.tile([P, width], F32, name=name)
+
+        def ts(dst, src, s1, op0, s2=None, op1=None):
+            if op1 is None:
+                nc.vector.tensor_scalar(out=dst, in0=src, scalar1=s1, scalar2=None, op0=op0)
+            else:
+                nc.vector.tensor_scalar(out=dst, in0=src, scalar1=s1, scalar2=s2, op0=op0, op1=op1)
+
+        def tt(dst, a, b):
+            nc.vector.tensor_tensor(out=dst, in0=a, in1=b, op=ALU.mult)
+
+        def largest(dst, src):
+            nc.vector.tensor_reduce(out=dst, in_=src, axis=AXIS.X, op=ALU.max, apply_absolute_value=True)
+
+        def invert(dst, src):
+            nc.vector.reciprocal(out=dst, in_=src)
+
+        def pivot_steps(name, matrix, pivots):
+            top, floor = column(name + "_top"), column(name + "_floor")
+            twice, sign = column(name + "_twice", H), column(name + "_sign", H)
+            bare, size, inverse = column(name + "_bare", H), column(name + "_size", H), column(name + "_inverse", H)
+            steps = [
+                (largest, (top[:], matrix)),
+                (ts, (twice[:], pivots, 0.0, ALU.is_ge, 2.0, ALU.mult)),
+                (ts, (floor[:], top[:], PIVOT_SHARE, ALU.mult, PIVOT_FLOOR, ALU.max)),
+                (ts, (sign[:], twice[:], 1.0, ALU.subtract)),
+                (tt, (bare[:], pivots, sign[:])),
+                (ts, (size[:], bare[:], floor[:], ALU.max)),
+                (invert, (inverse[:], size[:])),
+            ]
+            return steps, sign, size, inverse
+
+        l_steps, l_sign, l_size, l_inverse = pivot_steps("l", mixl_raw[:], mixl_raw[:, 0:4:3])
+        head1_scale, logit_scale, l_ratio = column("head1_scale"), column("logit_scale"), column("l_ratio", H)
+        l_steps = l_steps + [
+            (ts, (logit_scale[:], l_size[:, 0:1], 1.0 / math.sqrt(E), ALU.mult)),
+            (ts, (head1_scale[:], l_size[:, 1:2], l_sign[:, 1:2], ALU.mult, l_inverse[:, 0:1], ALU.mult)),
+            (ts, (l_ratio[:, 0:1], mixl_raw[:, 2:3], l_sign[:, 1:2], ALU.mult, l_inverse[:, 1:2], ALU.mult)),
+            (ts, (l_ratio[:, 1:2], mixl_raw[:, 1:2], l_sign[:, 0:1], ALU.mult, l_inverse[:, 0:1], ALU.mult)),
+        ]
+
+        w_steps, w_sign, w_size, w_inverse = pivot_steps("w", mixw_raw[:], mixw_raw[:, 2:4])
+        w_pivot, w_turned, w_ratio = column("w_pivot", H), column("w_turned", H), column("w_ratio", H)
+        key_gain = keep.tile([P, H, P, PACK], F32, name="key_gain")
+        gs_spread = gs_raw[:].rearrange("p (o t) -> p o t", o=1).to_broadcast([P, P, PACK])
+        w_steps = w_steps + [
+            (tt, (w_pivot[:], w_size[:], w_sign[:])),
+            (tt, (w_turned[:], mixw_raw[:, 0:2], w_sign[:])),
+            (ts, (key_gain[:, 0, :, :], gs_spread, w_pivot[:, 0:1], ALU.mult, math.sqrt(S), ALU.mult)),
+            (tt, (w_ratio[:], w_turned[:], w_inverse[:])),
+            (ts, (key_gain[:, 1, :, :], gs_spread, w_pivot[:, 1:2], ALU.mult, math.sqrt(S), ALU.mult)),
+        ]
 
         def turn_k_steps(b, h, engine):
             banks = ["m0", "m1", "o0", "o1"]
@@ -101,7 +155,13 @@ def tile_caittalkingheadsattention_t_kernel(tc, q, k, v_bytes, v_scale, mixl, mi
                     steps.append((turn_k, (b, h, c, t, e0, banks[c], engine)))
             return steps
 
-        k_bank, inv_sum, factors = {}, {}, {}
+        k_bank, inv_sum, exp_bias = {}, {}, {}
+
+        def scale_rows(engine, dst, src, factor):
+            if engine is nc.scalar:
+                nc.scalar.activation(out=dst, in_=src, func=ACT.Copy, scale=factor)
+            else:
+                ts(dst, src, factor, ALU.mult)
 
         def copy(engine, dst, src):
             if engine is nc.scalar:
@@ -117,7 +177,10 @@ def tile_caittalkingheadsattention_t_kernel(tc, q, k, v_bytes, v_scale, mixl, mi
             )
             if t == PACK - 1:
                 k_turned[b, h, c] = keep.tile([P, S], BF16, name="k_turned_%d%d%d" % (b, h, c))
-                copy(engine, k_turned[b, h, c][:], k_bank[b, h, c][:])
+                if h == 1:
+                    copy(engine, k_turned[b, h, c][:], k_bank[b, h, c][:])
+                else:
+                    scale_rows(engine, k_turned[b, h, c][:], k_bank[b, h, c][:], l_sign[:, 0:1])
 
         def turn_q(n, c):
             if c == 0:
@@ -144,20 +207,18 @@ def tile_caittalkingheadsattention_t_kernel(tc, q, k, v_bytes, v_scale, mixl, mi
             )
 
         def scale_head1(n):
-            scaled[n] = ring2.tile([P, H, S], F32, name="scaled")
-            for j in range(H):
-                nc.scalar.activation(
-                    out=scaled[n][:, j, :], in_=l_bank[n, 1][:], func=ACT.Copy, scale=logit_mix[:, H + j : H + j + 1]
-                )
+            scaled[n] = ring2.tile([P, S], F32, name="scaled")
+            scale_rows(nc.scalar, scaled[n][:], l_bank[n, 1][:], head1_scale[:])
 
         def mix_logits(n):
             logits[n] = ring2.tile([P, H, S], F32, name="logits")
+            operands = [scaled[n][:], l_bank[n, 0][:]]
             for j in range(H):
                 nc.vector.scalar_tensor_tensor(
                     out=logits[n][:, j, :],
-                    in0=l_bank[n, 0][:],
-                    scalar=logit_mix[:, j : j + 1],
-                    in1=scaled[n][:, j, :],
+                    in0=operands[j],
+                    scalar=l_ratio[:, j : j + 1],
+                    in1=operands[1 - j],
                     op0=ALU.mult,
                     op1=ALU.add,
                 )
@@ -165,6 +226,10 @@ def tile_caittalkingheadsattention_t_kernel(tc, q, k, v_bytes, v_scale, mixl, mi
         def row_max(n):
             neg_max[n] = ring3.tile([P, H], F32, name="neg_max")
             nc.vector.tensor_reduce(out=neg_max[n][:], in_=logits[n][:], axis=AXIS.X, op=ALU.max, negate=True)
+
+        def scale_bias(n):
+            exp_bias[n] = ring3.tile([P, H], F32, name="exp_bias")
+            scale_rows(nc.scalar, exp_bias[n][:], neg_max[n][:], logit_scale[:])
 
         def exponentials(n):
             expo[n] = ring2.tile([P, H, S], F32, name="expo")
@@ -174,7 +239,8 @@ def tile_caittalkingheadsattention_t_kernel(tc, q, k, v_bytes, v_scale, mixl, mi
                     out=expo[n][:, h, :],
                     in_=logits[n][:, h, :],
                     func=ACT.Exp,
-                    bias=neg_max[n][:, h : h + 1],
+                    bias=exp_bias[n][:, h : h + 1],
+                    scale=logit_scale[:],
                     accum_out=sums[n][:, h : h + 1],
                 )
 
@@ -182,43 +248,35 @@ def tile_caittalkingheadsattention_t_kernel(tc, q, k, v_bytes, v_scale, mixl, mi
             inv_sum[n] = ring3.tile([P, H], F32, name="inv_sum")
             nc.vector.reciprocal(out=inv_sum[n][:], in_=sums[n][:])
 
-        def share_factors(n):
-            factors[n] = ring3.tile([P, H, H], F32, name="factors")
-            nc.vector.tensor_tensor(
-                out=factors[n][:],
-                in0=weight_mix[:].rearrange("p (h j) -> p h j", j=H),
-                in1=inv_sum[n][:].rearrange("p (h o) -> p h o", o=1).to_broadcast([P, H, H]),
-                op=ALU.mult,
+        def weigh_head0(n, j, engine):
+            shares[n, j, 0] = ring3.tile([P, S], F32, name="share_%d" % j)
+            engine.tensor_scalar(
+                out=shares[n, j, 0][:],
+                in0=expo[n][:, 0, :],
+                scalar1=inv_sum[n][:, 0:1],
+                scalar2=w_ratio[:, j : j + 1],
+                op0=ALU.mult,
+                op1=ALU.mult,
             )
 
-        def weigh_head(n, j, h, engine):
-            shares[n, j, h] = ring2.tile([P, S], F32, name="share_%d%d" % (j, h))
-            if engine is nc.vector:
-                nc.vector.tensor_scalar(
-                    out=shares[n, j, h][:],
-                    in0=expo[n][:, h, :],
-                    scalar1=inv_sum[n][:, h : h + 1],
-                    scalar2=weight_mix[:, H * h + j : H * h + j + 1],
-                    op0=ALU.mult,
-                    op1=ALU.mult,
-                )
-            elif engine is nc.scalar:
-                nc.scalar.activation(
-                    out=shares[n, j, h][:], in_=expo[n][:, h, :], func=ACT.Copy, scale=factors[n][:, h, j : j + 1]
-                )
+        def weigh_head1(n, engine):
+            shares[n, 0, 1] = ring3.tile([P, S], F32, name="share_both")
+            shares[n, 1, 1] = shares[n, 0, 1]
+            if engine is nc.scalar:
+                scale_rows(nc.scalar, shares[n, 0, 1][:], expo[n][:, 1, :], inv_sum[n][:, 1:2])
             else:
                 nc.gpsimd.tensor_scalar(
-                    out=shares[n, j, h][:],
-                    in0=expo[n][:, h, :],
-                    scalar1=factors[n][:, h, j : j + 1],
+                    out=shares[n, 0, 1][:],
+                    in0=expo[n][:, 1, :],
+                    scalar1=inv_sum[n][:, 1:2],
                     scalar2=0.0,
                     op0=ALU.mult,
                     op1=ALU.add,
                 )
 
-        def turn_share(n, j, t, h):
+        def turn_share(n, j, t, h, bank):
             if t == 0 and h == 0:
-                mix_bank[n, j] = psum.tile([P, PACK, P], F32, name="mix_bank", tag="m%d" % j)
+                mix_bank[n, j] = psum.tile([P, PACK, P], F32, name="mix_bank", tag=bank, bufs=2 if bank == "q" else 1)
             nc.tensor.matmul(
                 mix_bank[n, j][:, t, :],
                 lhsT=shares[n, j, h][:, t * P : (t + 1) * P],
@@ -234,7 +292,7 @@ def tile_caittalkingheadsattention_t_kernel(tc, q, k, v_bytes, v_scale, mixl, mi
             nc.vector.tensor_tensor(
                 out=u_wide[n][:, j, :, :],
                 in0=mix_bank[n, j][:].rearrange("p t n -> p n t"),
-                in1=key_gain[:],
+                in1=key_gain[:, j, :, :],
                 op=ALU.mult,
             )
 
@@ -247,10 +305,10 @@ def tile_caittalkingheadsattention_t_kernel(tc, q, k, v_bytes, v_scale, mixl, mi
                 in_=u_wide[n][:].rearrange("p j n t -> p (j n t)"),
             )
 
-        def mix_values(n):
+        def mix_values(n, banks=("o0", "o1")):
             b = n // TILES_PER_BATCH
             for j in range(H):
-                out_bank[n, j] = psum.tile([P, E], F32, name="out_bank", tag="o%d" % j)
+                out_bank[n, j] = psum.tile([P, E], F32, name="out_bank", tag=banks[j], bufs=2 if banks[j] == "q" else 1)
                 nc.tensor.matmul_mx(
                     out=out_bank[n, j][:],
                     lhsT=u_codes[n][:, j * P : (j + 1) * P].bitcast(FP8X4),
@@ -263,7 +321,7 @@ def tile_caittalkingheadsattention_t_kernel(tc, q, k, v_bytes, v_scale, mixl, mi
 
         def store(n):
             result = ring3.tile([P, H, E], F32, name="result")
-            if n < N_TILES - 1:
+            if n < N_TILES - 2:
                 for j in range(H):
                     nc.scalar.copy(out=result[:, j, :], in_=out_bank[n, j][:])
                 nc.sync.dma_start(out=token_rows(out, n), in_=result[:])
@@ -272,32 +330,31 @@ def tile_caittalkingheadsattention_t_kernel(tc, q, k, v_bytes, v_scale, mixl, mi
                     copy(engine, result[:, j, :], out_bank[n, j][:])
                     nc.sync.dma_start(out=token_rows(out, n)[:, j, :], in_=result[:, j, :])
 
-        def widen_v(b, j, engine):
+        def widen_v_steps(b, j, engine):
             v_wide[b, j] = ring2.tile([P, PACK, E], BF16, name="v_wide")
-            for t in range(PACK):
-                codes = v_raw[b][:, j, t * E : (t + 1) * E].bitcast(FP8)
-                if engine is nc.scalar:
-                    nc.scalar.activation(
-                        out=v_wide[b, j][:, t, :], in_=codes, func=ACT.Copy, scale=v_row_scale[:, t : t + 1]
-                    )
-                else:
-                    nc.vector.tensor_scalar(
-                        out=v_wide[b, j][:, t, :],
-                        in0=codes,
-                        scalar1=v_row_scale[:, t : t + 1],
-                        scalar2=None,
-                        op0=ALU.mult,
-                    )
+            return [
+                (
+                    scale_rows,
+                    (
+                        engine,
+                        v_wide[b, j][:, t, :],
+                        v_raw[b][:, j, t * E : (t + 1) * E].bitcast(FP8),
+                        v_row_scale[:, t : t + 1],
+                    ),
+                )
+                for t in range(PACK)
+            ]
 
-        def weave_v(b, j, engine):
-            v_woven[b, j] = ring2.tile([P, E, PACK], BF16, name="v_woven", align_bytes=64)
-            planes = v_wide[b, j][:].rearrange("p t e -> p e t")
+        def weave_v(b, j, engine, e0=0, e1=E):
+            if e0 == 0:
+                v_woven[b, j] = ring2.tile([P, E, PACK], BF16, name="v_woven", align_bytes=64)
+            planes = v_wide[b, j][:, :, e0:e1].rearrange("p t e -> p e t")
             if engine is nc.gpsimd:
                 nc.gpsimd.tensor_scalar(
-                    out=v_woven[b, j][:], in0=planes, scalar1=1.0, scalar2=0.0, op0=ALU.mult, op1=ALU.add
+                    out=v_woven[b, j][:, e0:e1, :], in0=planes, scalar1=1.0, scalar2=0.0, op0=ALU.mult, op1=ALU.add
                 )
             else:
-                nc.vector.tensor_copy(out=v_woven[b, j][:], in_=planes)
+                nc.vector.tensor_copy(out=v_woven[b, j][:, e0:e1, :], in_=planes)
 
         def quantise_v(b, j):
             v_codes[b, j] = keep.tile([P, E], U32, name="v_codes_%d%d" % (b, j), align_bytes=64)
@@ -318,54 +375,47 @@ def tile_caittalkingheadsattention_t_kernel(tc, q, k, v_bytes, v_scale, mixl, mi
         for i in range(WARM_MATMULS):
             nc.tensor.matmul(warm_bank[:], lhsT=warm_rows[:, :P], rhs=warm_rows[:], start=True, stop=True)
 
+        for pair in zip(l_steps, w_steps):
+            run(pair)
+        run(w_steps[len(l_steps) :])
         for c in range(PACK):
             turn_q(0, c)
         copy_q(0)
         first_k = turn_k_steps(0, 1, nc.scalar) + turn_k_steps(0, 0, nc.scalar)
         run(first_k[: 2 * PACK])
-        nc.vector.tensor_scalar(
-            out=logit_mix[:], in0=mixl_raw[:], scalar1=1.0 / math.sqrt(E), scalar2=None, op0=ALU.mult
-        )
         for c in range(PACK):
             turn_q(1, c)
         for j in range(H):
-            widen_v(0, j, nc.vector)
+            run(widen_v_steps(0, j, nc.vector))
         for j in range(H):
             weave_v(0, j, nc.vector)
         for j in range(H):
             quantise_v(0, j)
-        nc.vector.tensor_copy(out=weight_mix[:], in_=mixw_raw[:])
-        nc.vector.tensor_scalar(
-            out=key_gain[:],
-            in0=gs_raw[:].rearrange("p (o t) -> p o t", o=1).to_broadcast([P, P, PACK]),
-            scalar1=math.sqrt(S),
-            scalar2=None,
-            op0=ALU.mult,
-        )
-        k_jobs = {1: (1, 1, nc.scalar), 2: (1, 0, nc.scalar)}
+        k_jobs = {1: (1, 0, nc.vector), 3: (1, 1, nc.scalar)}
 
-        for n in range(N_TILES + 4):
-            draining = n >= N_TILES
+        def turn_share_steps(m, banks=("m0", "m1")):
+            return [(turn_share, (m, j, t, h, banks[j])) for j in range(H) for t in range(PACK) for h in range(H)]
+
+        for n in range(N_TILES):
             if live(n + 4):
                 load_q(n + 4)
             if live(n - 1):
                 row_max(n - 1)
-            if live(n + 1):
-                copy_q(n + 1)
-            if live(n - 4):
-                quantise_u(n - 4)
+            if n == 0:
+                copy_q(1)
+            if live(n - OUT_LAG):
+                quantise_u(n - OUT_LAG)
             if n == 2:
-                weave_v(1, 1, nc.vector)
+                quantise_v(1, 0)
             if n == 3:
+                weave_v(1, 1, nc.vector)
+            if n == 4:
                 quantise_v(1, 1)
             if live(n - 2):
-                weigh_head(n - 2, 0, 0, nc.vector)
-                share_factors(n - 2)
-                if draining:
-                    weigh_head(n - 2, 1, 0, nc.vector)
-                else:
-                    for j, h in [(0, 1), (1, 0), (1, 1)]:
-                        weigh_head(n - 2, j, h, nc.gpsimd)
+                invert_sums(n - 2)
+                weigh_head0(n - 2, 0, nc.gpsimd)
+                weigh_head1(n - 2, nc.gpsimd)
+                weigh_head0(n - 2, 1, nc.gpsimd)
 
             steps = []
             if live(n + 2):
@@ -374,40 +424,80 @@ def tile_caittalkingheadsattention_t_kernel(tc, q, k, v_bytes, v_scale, mixl, mi
                 steps = first_k[2 * PACK :] + steps
             if n in k_jobs:
                 steps = turn_k_steps(*k_jobs[n]) + steps
-            if live(n - 3):
-                steps = steps + [(turn_share, (n - 3, j, t, h)) for j in range(H) for t in range(PACK) for h in range(H)]
+            m = n - MIX_LAG
+            if live(m):
+                steps = steps + turn_share_steps(m)
             per_gap = 4 if n == 0 else 3
             gaps = [steps[g * per_gap : (g + 1) * per_gap] for g in range(2 * PACK)]
             for c in range(PACK):
-                if live(n):
-                    logit_pass(n, 1, c)
-                    if c == PACK - 1:
-                        scale_head1(n)
+                logit_pass(n, 1, c)
+                if c == PACK - 1:
+                    scale_head1(n)
                 run(gaps[c])
-            if live(n - 3):
-                apply_gain(n - 3, 0)
+            if live(n - 1):
+                scale_bias(n - 1)
+            if n > 0 and live(n + 1):
+                copy_q(n + 1)
+            if live(m):
+                apply_gain(m, 0)
             for c in range(PACK):
-                if live(n):
-                    logit_pass(n, 0, c)
+                logit_pass(n, 0, c)
                 run(gaps[PACK + c])
             if live(n - 1):
                 exponentials(n - 1)
-            if draining and live(n - 2):
-                weigh_head(n - 2, 0, 1, nc.scalar)
-                weigh_head(n - 2, 1, 1, nc.scalar)
-            if live(n):
-                mix_logits(n)
-            if live(n - 4):
-                mix_values(n - 4)
-            if live(n - 3):
-                apply_gain(n - 3, 1)
-            if n == 1:
-                widen_v(1, 1, nc.vector)
-                quantise_v(1, 0)
-            if live(n - 1):
-                invert_sums(n - 1)
-            if live(n - 4):
-                store(n - 4)
+            mix_logits(n)
+            if live(n - OUT_LAG):
+                mix_values(n - OUT_LAG)
+            if live(m):
+                apply_gain(m, 1)
+            if live(n - OUT_LAG):
+                store(n - OUT_LAG)
             if n == 0:
-                widen_v(1, 0, nc.scalar)
+                run(widen_v_steps(1, 0, nc.scalar))
                 weave_v(1, 0, nc.gpsimd)
+            if n == 1:
+                last_v = widen_v_steps(1, 1, nc.scalar)
+                run(last_v[:2])
+            if n == 2:
+                run(last_v[2:])
+
+        last = N_TILES - 1
+
+        row_max(last)
+        quantise_u(last - 4)
+        invert_sums(last - 1)
+        scale_bias(last)
+        run(turn_share_steps(last - 3))
+        apply_gain(last - 3, 0)
+        weigh_head0(last - 1, 0, nc.vector)
+        weigh_head0(last - 1, 1, nc.vector)
+        exponentials(last)
+        weigh_head1(last - 1, nc.scalar)
+        mix_values(last - 4)
+        run(turn_share_steps(last - 2, ("q", "q")))
+        apply_gain(last - 3, 1)
+        invert_sums(last)
+        weigh_head1(last, nc.scalar)
+        store(last - 4)
+        apply_gain(last - 2, 0)
+        weigh_head0(last, 0, nc.vector)
+        weigh_head0(last, 1, nc.vector)
+        quantise_u(last - 3)
+        run(turn_share_steps(last - 1, ("l1", "l0")))
+        mix_values(last - 3)
+        store(last - 3)
+        run(turn_share_steps(last))
+        apply_gain(last - 2, 1)
+        apply_gain(last - 1, 0)
+        quantise_u(last - 2)
+        mix_values(last - 2)
+        store(last - 2)
+        apply_gain(last - 1, 1)
+        apply_gain(last, 0)
+        quantise_u(last - 1)
+        mix_values(last - 1, ("q", "q"))
+        apply_gain(last, 1)
+        quantise_u(last)
+        mix_values(last, ("l1", "l0"))
+        store(last - 1)
+        store(last)

@@ -19,13 +19,24 @@ AXIS = mybir.AxisListType
 
 P = 128
 PACK = 4
+CHUNKS = E // P
 TILES_PER_BATCH = T // P
 N_TILES = B * TILES_PER_BATCH
-WARM_MATMULS = 6
+
+Q_LOAD_AHEAD = 4
+Q_TURN_AHEAD = 2
+SHARE_LAG = 2
 MIX_LAG = 4
 OUT_LAG = 5
+TURNS_PER_GAP = 3
+
 PIVOT_SHARE = 2.0**-40
 PIVOT_FLOOR = 2.0**-100
+
+Q_BANKS = ("q", "q")
+LOGIT_BANKS = ("l0", "l1")
+MIX_BANKS = ("m0", "m1")
+OUT_BANKS = ("o0", "o1")
 
 
 def tile_caittalkingheadsattention_t_kernel(tc, q, k, v_bytes, v_scale, mixl, mixw, gs, out):
@@ -38,12 +49,40 @@ def tile_caittalkingheadsattention_t_kernel(tc, q, k, v_bytes, v_scale, mixl, mi
         psum = ctx.enter_context(tc.psum_pool(name="psum", bufs=1))
         ctx.enter_context(tc.manual_schedule())
 
-        q_rows, q_bank, q_turned, scaled, logits, neg_max, expo, sums = {}, {}, {}, {}, {}, {}, {}, {}
-        shares, u_wide, u_codes, u_scales, mix_bank, out_bank, l_bank = {}, {}, {}, {}, {}, {}, {}
-        k_rows, k_turned, v_raw, v_wide, v_woven, v_codes, v_scales = {}, {}, {}, {}, {}, {}, {}
+        q_rows, q_bank, q_turned, l_bank, head1_logits, logits = {}, {}, {}, {}, {}, {}
+        neg_max, exp_bias, expo, sums, inv_sum, shares = {}, {}, {}, {}, {}, {}
+        mix_bank, u_wide, u_codes, u_scales, out_bank = {}, {}, {}, {}, {}
+        k_rows, k_bank, k_turned = {}, {}, {}
+        v_raw, v_planes, v_woven, v_codes, v_scales = {}, {}, {}, {}, {}
 
         def live(n):
             return 0 <= n < N_TILES
+
+        def bank_tile(shape, dtype, name, tag):
+            return psum.tile(shape, dtype, name=name, tag=tag, bufs=2 if tag in Q_BANKS else 1)
+
+        def run(steps):
+            for fn, args in steps:
+                fn(*args)
+
+        def copy(engine, dst, src):
+            if engine is nc.scalar:
+                nc.scalar.copy(out=dst, in_=src)
+            else:
+                engine.tensor_copy(out=dst, in_=src)
+
+        def scalar_ops(dst, src, s1, op0, s2=None, op1=None):
+            if op1 is None:
+                nc.vector.tensor_scalar(out=dst, in0=src, scalar1=s1, scalar2=None, op0=op0)
+            else:
+                nc.vector.tensor_scalar(out=dst, in0=src, scalar1=s1, scalar2=s2, op0=op0, op1=op1)
+
+        def scale_rows(engine, dst, src, factor):
+            if engine is nc.scalar:
+                nc.scalar.activation(out=dst, in_=src, func=ACT.Copy, scale=factor)
+            else:
+                scalar_ops(dst, src, factor, ALU.mult)
+
 
         def token_rows(dram, n):
             b, i = divmod(n, TILES_PER_BATCH)
@@ -86,24 +125,14 @@ def tile_caittalkingheadsattention_t_kernel(tc, q, k, v_bytes, v_scale, mixl, mi
         make_identity(nc, ident_bf16[:])
         make_identity(nc, ident_f32[:])
 
-        warm_in = keep.tile([P, 1], F32, name="warm_in")
-        warm_out = keep.tile([P, 1], F32, name="warm_out")
-        nc.vector.memset(warm_in[:], 0.0)
-        nc.scalar.activation(out=warm_out[:], in_=warm_in[:], func=ACT.Exp)
 
         def column(name, width=1):
             return keep.tile([P, width], F32, name=name)
 
-        def ts(dst, src, s1, op0, s2=None, op1=None):
-            if op1 is None:
-                nc.vector.tensor_scalar(out=dst, in0=src, scalar1=s1, scalar2=None, op0=op0)
-            else:
-                nc.vector.tensor_scalar(out=dst, in0=src, scalar1=s1, scalar2=s2, op0=op0, op1=op1)
-
-        def tt(dst, a, b):
+        def multiply(dst, a, b):
             nc.vector.tensor_tensor(out=dst, in0=a, in1=b, op=ALU.mult)
 
-        def largest(dst, src):
+        def largest_magnitude(dst, src):
             nc.vector.tensor_reduce(out=dst, in_=src, axis=AXIS.X, op=ALU.max, apply_absolute_value=True)
 
         def invert(dst, src):
@@ -114,12 +143,12 @@ def tile_caittalkingheadsattention_t_kernel(tc, q, k, v_bytes, v_scale, mixl, mi
             twice, sign = column(name + "_twice", H), column(name + "_sign", H)
             bare, size, inverse = column(name + "_bare", H), column(name + "_size", H), column(name + "_inverse", H)
             steps = [
-                (largest, (top[:], matrix)),
-                (ts, (twice[:], pivots, 0.0, ALU.is_ge, 2.0, ALU.mult)),
-                (ts, (floor[:], top[:], PIVOT_SHARE, ALU.mult, PIVOT_FLOOR, ALU.max)),
-                (ts, (sign[:], twice[:], 1.0, ALU.subtract)),
-                (tt, (bare[:], pivots, sign[:])),
-                (ts, (size[:], bare[:], floor[:], ALU.max)),
+                (largest_magnitude, (top[:], matrix)),
+                (scalar_ops, (twice[:], pivots, 0.0, ALU.is_ge, 2.0, ALU.mult)),
+                (scalar_ops, (floor[:], top[:], PIVOT_SHARE, ALU.mult, PIVOT_FLOOR, ALU.max)),
+                (scalar_ops, (sign[:], twice[:], 1.0, ALU.subtract)),
+                (multiply, (bare[:], pivots, sign[:])),
+                (scalar_ops, (size[:], bare[:], floor[:], ALU.max)),
                 (invert, (inverse[:], size[:])),
             ]
             return steps, sign, size, inverse
@@ -127,53 +156,32 @@ def tile_caittalkingheadsattention_t_kernel(tc, q, k, v_bytes, v_scale, mixl, mi
         l_steps, l_sign, l_size, l_inverse = pivot_steps("l", mixl_raw[:], mixl_raw[:, 0:4:3])
         head1_scale, logit_scale, l_ratio = column("head1_scale"), column("logit_scale"), column("l_ratio", H)
         l_steps = l_steps + [
-            (ts, (logit_scale[:], l_size[:, 0:1], 1.0 / math.sqrt(E), ALU.mult)),
-            (ts, (head1_scale[:], l_size[:, 1:2], l_sign[:, 1:2], ALU.mult, l_inverse[:, 0:1], ALU.mult)),
-            (ts, (l_ratio[:, 0:1], mixl_raw[:, 2:3], l_sign[:, 1:2], ALU.mult, l_inverse[:, 1:2], ALU.mult)),
-            (ts, (l_ratio[:, 1:2], mixl_raw[:, 1:2], l_sign[:, 0:1], ALU.mult, l_inverse[:, 0:1], ALU.mult)),
+            (scalar_ops, (logit_scale[:], l_size[:, 0:1], 1.0 / math.sqrt(E), ALU.mult)),
+            (scalar_ops, (head1_scale[:], l_size[:, 1:2], l_sign[:, 1:2], ALU.mult, l_inverse[:, 0:1], ALU.mult)),
+            (scalar_ops, (l_ratio[:, 0:1], mixl_raw[:, 2:3], l_sign[:, 1:2], ALU.mult, l_inverse[:, 1:2], ALU.mult)),
+            (scalar_ops, (l_ratio[:, 1:2], mixl_raw[:, 1:2], l_sign[:, 0:1], ALU.mult, l_inverse[:, 0:1], ALU.mult)),
         ]
 
         w_steps, w_sign, w_size, w_inverse = pivot_steps("w", mixw_raw[:], mixw_raw[:, 2:4])
-        w_pivot, w_turned, w_ratio = column("w_pivot", H), column("w_turned", H), column("w_ratio", H)
+        w_pivot, w_signed, w_ratio = column("w_pivot", H), column("w_signed", H), column("w_ratio", H)
         key_gain = keep.tile([P, H, P, PACK], F32, name="key_gain")
         gs_spread = gs_raw[:].rearrange("p (o t) -> p o t", o=1).to_broadcast([P, P, PACK])
         w_steps = w_steps + [
-            (tt, (w_pivot[:], w_size[:], w_sign[:])),
-            (tt, (w_turned[:], mixw_raw[:, 0:2], w_sign[:])),
-            (ts, (key_gain[:, 0, :, :], gs_spread, w_pivot[:, 0:1], ALU.mult, math.sqrt(S), ALU.mult)),
-            (tt, (w_ratio[:], w_turned[:], w_inverse[:])),
-            (ts, (key_gain[:, 1, :, :], gs_spread, w_pivot[:, 1:2], ALU.mult, math.sqrt(S), ALU.mult)),
+            (multiply, (w_pivot[:], w_size[:], w_sign[:])),
+            (multiply, (w_signed[:], mixw_raw[:, 0:2], w_sign[:])),
+            (scalar_ops, (key_gain[:, 0, :, :], gs_spread, w_pivot[:, 0:1], ALU.mult, math.sqrt(S), ALU.mult)),
+            (multiply, (w_ratio[:], w_signed[:], w_inverse[:])),
+            (scalar_ops, (key_gain[:, 1, :, :], gs_spread, w_pivot[:, 1:2], ALU.mult, math.sqrt(S), ALU.mult)),
         ]
 
-        def turn_k_steps(b, h, engine):
-            banks = ["m0", "m1", "o0", "o1"]
-            steps = []
-            for c in range(PACK):
-                half, parity = divmod(c, 2)
-                e0 = 256 * half + parity
-                for t in range(PACK):
-                    steps.append((turn_k, (b, h, c, t, e0, banks[c], engine)))
-            return steps
 
-        k_bank, inv_sum, exp_bias = {}, {}, {}
-
-        def scale_rows(engine, dst, src, factor):
-            if engine is nc.scalar:
-                nc.scalar.activation(out=dst, in_=src, func=ACT.Copy, scale=factor)
-            else:
-                ts(dst, src, factor, ALU.mult)
-
-        def copy(engine, dst, src):
-            if engine is nc.scalar:
-                nc.scalar.copy(out=dst, in_=src)
-            else:
-                engine.tensor_copy(out=dst, in_=src)
-
-        def turn_k(b, h, c, t, e0, bank, engine):
+        def turn_k(b, h, c, t, engine):
             if t == 0:
-                k_bank[b, h, c] = psum.tile([P, S], BF16, name="k_bank", tag=bank)
+                k_bank[b, h, c] = bank_tile([P, S], BF16, "k_bank", (MIX_BANKS + OUT_BANKS)[c])
+            half, parity = divmod(c, 2)
+            e0 = 2 * P * half + parity
             nc.tensor.transpose(
-                k_bank[b, h, c][:, t * P : (t + 1) * P], k_rows[b, h][:, t, e0 : e0 + 255 : 2], ident_bf16[:]
+                k_bank[b, h, c][:, t * P : (t + 1) * P], k_rows[b, h][:, t, e0 : e0 + 2 * P - 1 : 2], ident_bf16[:]
             )
             if t == PACK - 1:
                 k_turned[b, h, c] = keep.tile([P, S], BF16, name="k_turned_%d%d%d" % (b, h, c))
@@ -182,19 +190,26 @@ def tile_caittalkingheadsattention_t_kernel(tc, q, k, v_bytes, v_scale, mixl, mi
                 else:
                     scale_rows(engine, k_turned[b, h, c][:], k_bank[b, h, c][:], l_sign[:, 0:1])
 
-        def turn_q(n, c):
-            if c == 0:
-                q_bank[n] = psum.tile([P, PACK, P], F32, name="q_bank", tag="q", bufs=2)
+        def turn_k_steps(b, h, engine):
+            return [(turn_k, (b, h, c, t, engine)) for c in range(CHUNKS) for t in range(PACK)]
+
+        def turn_q(n, group):
+            if group == 0:
+                q_bank[n] = bank_tile([P, 2 * H, P], F32, "q_bank", Q_BANKS[0])
             words = q_rows[n][:].rearrange("p h e -> p (h e)").bitcast(F32)
-            nc.tensor.transpose(q_bank[n][:, c, :], words[:, c * P : (c + 1) * P], ident_f32[:])
+            nc.tensor.transpose(q_bank[n][:, group, :], words[:, group * P : (group + 1) * P], ident_f32[:])
+
+        def turn_q_steps(n):
+            return [(turn_q, (n, group)) for group in range(2 * H)]
 
         def copy_q(n):
-            q_turned[n] = ring2.tile([P, PACK * P], F32, name="q_turned")
-            nc.scalar.copy(out=q_turned[n][:], in_=q_bank[n][:].rearrange("p c n -> p (c n)"))
+            q_turned[n] = ring2.tile([P, 2 * H * P], F32, name="q_turned")
+            nc.scalar.copy(out=q_turned[n][:], in_=q_bank[n][:].rearrange("p g n -> p (g n)"))
+
 
         def logit_pass(n, h, c):
             if c == 0:
-                l_bank[n, h] = psum.tile([P, S], F32, name="l_bank", tag="l%d" % h)
+                l_bank[n, h] = bank_tile([P, S], F32, "l_bank", LOGIT_BANKS[h])
             half, parity = divmod(c, 2)
             col0 = (2 * h + half) * 2 * P + parity
             pairs = q_turned[n][:].bitcast(BF16)
@@ -203,22 +218,22 @@ def tile_caittalkingheadsattention_t_kernel(tc, q, k, v_bytes, v_scale, mixl, mi
                 lhsT=pairs[:, col0 : col0 + 2 * P - 1 : 2],
                 rhs=k_turned[n // TILES_PER_BATCH, h, c][:],
                 start=(c == 0),
-                stop=(c == PACK - 1),
+                stop=(c == CHUNKS - 1),
             )
 
         def scale_head1(n):
-            scaled[n] = ring2.tile([P, S], F32, name="scaled")
-            scale_rows(nc.scalar, scaled[n][:], l_bank[n, 1][:], head1_scale[:])
+            head1_logits[n] = ring2.tile([P, S], F32, name="head1_logits")
+            scale_rows(nc.scalar, head1_logits[n][:], l_bank[n, 1][:], head1_scale[:])
 
         def mix_logits(n):
             logits[n] = ring2.tile([P, H, S], F32, name="logits")
-            operands = [scaled[n][:], l_bank[n, 0][:]]
+            terms = [l_bank[n, 0][:], head1_logits[n][:]]
             for j in range(H):
                 nc.vector.scalar_tensor_tensor(
                     out=logits[n][:, j, :],
-                    in0=operands[j],
+                    in0=terms[1 - j],
                     scalar=l_ratio[:, j : j + 1],
-                    in1=operands[1 - j],
+                    in1=terms[j],
                     op0=ALU.mult,
                     op1=ALU.add,
                 )
@@ -246,9 +261,9 @@ def tile_caittalkingheadsattention_t_kernel(tc, q, k, v_bytes, v_scale, mixl, mi
 
         def invert_sums(n):
             inv_sum[n] = ring3.tile([P, H], F32, name="inv_sum")
-            nc.vector.reciprocal(out=inv_sum[n][:], in_=sums[n][:])
+            invert(inv_sum[n][:], sums[n][:])
 
-        def weigh_head0(n, j, engine):
+        def share_head0(n, j, engine):
             shares[n, j, 0] = ring3.tile([P, S], F32, name="share_%d" % j)
             engine.tensor_scalar(
                 out=shares[n, j, 0][:],
@@ -259,7 +274,7 @@ def tile_caittalkingheadsattention_t_kernel(tc, q, k, v_bytes, v_scale, mixl, mi
                 op1=ALU.mult,
             )
 
-        def weigh_head1(n, engine):
+        def share_head1(n, engine):
             shares[n, 0, 1] = ring3.tile([P, S], F32, name="share_both")
             shares[n, 1, 1] = shares[n, 0, 1]
             if engine is nc.scalar:
@@ -274,9 +289,9 @@ def tile_caittalkingheadsattention_t_kernel(tc, q, k, v_bytes, v_scale, mixl, mi
                     op1=ALU.add,
                 )
 
-        def turn_share(n, j, t, h, bank):
+        def turn_share(n, j, t, h, tag):
             if t == 0 and h == 0:
-                mix_bank[n, j] = psum.tile([P, PACK, P], F32, name="mix_bank", tag=bank, bufs=2 if bank == "q" else 1)
+                mix_bank[n, j] = bank_tile([P, PACK, P], F32, "mix_bank", tag)
             nc.tensor.matmul(
                 mix_bank[n, j][:, t, :],
                 lhsT=shares[n, j, h][:, t * P : (t + 1) * P],
@@ -285,6 +300,9 @@ def tile_caittalkingheadsattention_t_kernel(tc, q, k, v_bytes, v_scale, mixl, mi
                 start=(h == 0),
                 stop=(h == H - 1),
             )
+
+        def turn_share_steps(n, tags=MIX_BANKS):
+            return [(turn_share, (n, j, t, h, tags[j])) for j in range(H) for t in range(PACK) for h in range(H)]
 
         def apply_gain(n, j):
             if j == 0:
@@ -305,10 +323,10 @@ def tile_caittalkingheadsattention_t_kernel(tc, q, k, v_bytes, v_scale, mixl, mi
                 in_=u_wide[n][:].rearrange("p j n t -> p (j n t)"),
             )
 
-        def mix_values(n, banks=("o0", "o1")):
+        def mix_values(n, tags=OUT_BANKS):
             b = n // TILES_PER_BATCH
             for j in range(H):
-                out_bank[n, j] = psum.tile([P, E], F32, name="out_bank", tag=banks[j], bufs=2 if banks[j] == "q" else 1)
+                out_bank[n, j] = bank_tile([P, E], F32, "out_bank", tags[j])
                 nc.tensor.matmul_mx(
                     out=out_bank[n, j][:],
                     lhsT=u_codes[n][:, j * P : (j + 1) * P].bitcast(FP8X4),
@@ -321,23 +339,25 @@ def tile_caittalkingheadsattention_t_kernel(tc, q, k, v_bytes, v_scale, mixl, mi
 
         def store(n):
             result = ring3.tile([P, H, E], F32, name="result")
-            if n < N_TILES - 2:
-                for j in range(H):
-                    nc.scalar.copy(out=result[:, j, :], in_=out_bank[n, j][:])
-                nc.sync.dma_start(out=token_rows(out, n), in_=result[:])
-            else:
-                for j, engine in enumerate([nc.scalar, nc.vector]):
-                    copy(engine, result[:, j, :], out_bank[n, j][:])
-                    nc.sync.dma_start(out=token_rows(out, n)[:, j, :], in_=result[:, j, :])
+            for j in range(H):
+                nc.scalar.copy(out=result[:, j, :], in_=out_bank[n, j][:])
+            nc.sync.dma_start(out=token_rows(out, n), in_=result[:])
+
+        def store_by_head(n):
+            result = ring3.tile([P, H, E], F32, name="result")
+            for j, engine in enumerate([nc.scalar, nc.vector]):
+                copy(engine, result[:, j, :], out_bank[n, j][:])
+                nc.sync.dma_start(out=token_rows(out, n)[:, j, :], in_=result[:, j, :])
+
 
         def widen_v_steps(b, j, engine):
-            v_wide[b, j] = ring2.tile([P, PACK, E], BF16, name="v_wide")
+            v_planes[b, j] = ring2.tile([P, PACK, E], BF16, name="v_planes")
             return [
                 (
                     scale_rows,
                     (
                         engine,
-                        v_wide[b, j][:, t, :],
+                        v_planes[b, j][:, t, :],
                         v_raw[b][:, j, t * E : (t + 1) * E].bitcast(FP8),
                         v_row_scale[:, t : t + 1],
                     ),
@@ -345,16 +365,15 @@ def tile_caittalkingheadsattention_t_kernel(tc, q, k, v_bytes, v_scale, mixl, mi
                 for t in range(PACK)
             ]
 
-        def weave_v(b, j, engine, e0=0, e1=E):
-            if e0 == 0:
-                v_woven[b, j] = ring2.tile([P, E, PACK], BF16, name="v_woven", align_bytes=64)
-            planes = v_wide[b, j][:, :, e0:e1].rearrange("p t e -> p e t")
+        def weave_v(b, j, engine):
+            v_woven[b, j] = ring2.tile([P, E, PACK], BF16, name="v_woven", align_bytes=64)
+            planes = v_planes[b, j][:].rearrange("p t e -> p e t")
             if engine is nc.gpsimd:
                 nc.gpsimd.tensor_scalar(
-                    out=v_woven[b, j][:, e0:e1, :], in0=planes, scalar1=1.0, scalar2=0.0, op0=ALU.mult, op1=ALU.add
+                    out=v_woven[b, j][:], in0=planes, scalar1=1.0, scalar2=0.0, op0=ALU.mult, op1=ALU.add
                 )
             else:
-                nc.vector.tensor_copy(out=v_woven[b, j][:, e0:e1, :], in_=planes)
+                nc.vector.tensor_copy(out=v_woven[b, j][:], in_=planes)
 
         def quantise_v(b, j):
             v_codes[b, j] = keep.tile([P, E], U32, name="v_codes_%d%d" % (b, j), align_bytes=64)
@@ -365,44 +384,31 @@ def tile_caittalkingheadsattention_t_kernel(tc, q, k, v_bytes, v_scale, mixl, mi
                 in_=v_woven[b, j][:].rearrange("p e t -> p (e t)"),
             )
 
-        def run(steps):
-            for fn, args in steps:
-                fn(*args)
-
-        warm_rows = keep.tile([P, S], BF16, name="warm_rows")
-        nc.vector.memset(warm_rows[:], 0.0)
-        warm_bank = psum.tile([P, S], F32, name="warm_bank", tag="l0")
-        for i in range(WARM_MATMULS):
-            nc.tensor.matmul(warm_bank[:], lhsT=warm_rows[:, :P], rhs=warm_rows[:], start=True, stop=True)
-
         for pair in zip(l_steps, w_steps):
             run(pair)
         run(w_steps[len(l_steps) :])
-        for c in range(PACK):
-            turn_q(0, c)
+        run(turn_q_steps(0))
         copy_q(0)
         first_k = turn_k_steps(0, 1, nc.scalar) + turn_k_steps(0, 0, nc.scalar)
         run(first_k[: 2 * PACK])
-        for c in range(PACK):
-            turn_q(1, c)
+        run(turn_q_steps(1))
         for j in range(H):
             run(widen_v_steps(0, j, nc.vector))
         for j in range(H):
             weave_v(0, j, nc.vector)
         for j in range(H):
             quantise_v(0, j)
+
         k_jobs = {1: (1, 0, nc.vector), 3: (1, 1, nc.scalar)}
 
-        def turn_share_steps(m, banks=("m0", "m1")):
-            return [(turn_share, (m, j, t, h, banks[j])) for j in range(H) for t in range(PACK) for h in range(H)]
-
         for n in range(N_TILES):
-            if live(n + 4):
-                load_q(n + 4)
+            if live(n + Q_LOAD_AHEAD):
+                load_q(n + Q_LOAD_AHEAD)
             if live(n - 1):
                 row_max(n - 1)
             if n == 0:
                 copy_q(1)
+
             if live(n - OUT_LAG):
                 quantise_u(n - OUT_LAG)
             if n == 2:
@@ -411,57 +417,59 @@ def tile_caittalkingheadsattention_t_kernel(tc, q, k, v_bytes, v_scale, mixl, mi
                 weave_v(1, 1, nc.vector)
             if n == 4:
                 quantise_v(1, 1)
-            if live(n - 2):
-                invert_sums(n - 2)
-                weigh_head0(n - 2, 0, nc.gpsimd)
-                weigh_head1(n - 2, nc.gpsimd)
-                weigh_head0(n - 2, 1, nc.gpsimd)
+            if live(n - SHARE_LAG):
+                invert_sums(n - SHARE_LAG)
+                share_head0(n - SHARE_LAG, 0, nc.gpsimd)
+                share_head1(n - SHARE_LAG, nc.gpsimd)
+                share_head0(n - SHARE_LAG, 1, nc.gpsimd)
 
-            steps = []
-            if live(n + 2):
-                steps = [(turn_q, (n + 2, c)) for c in range(PACK)]
+            turns = []
             if n == 0:
-                steps = first_k[2 * PACK :] + steps
+                turns = first_k[2 * PACK :]
             if n in k_jobs:
-                steps = turn_k_steps(*k_jobs[n]) + steps
-            m = n - MIX_LAG
-            if live(m):
-                steps = steps + turn_share_steps(m)
-            per_gap = 4 if n == 0 else 3
-            gaps = [steps[g * per_gap : (g + 1) * per_gap] for g in range(2 * PACK)]
-            for c in range(PACK):
+                turns = turn_k_steps(*k_jobs[n])
+            if live(n + Q_TURN_AHEAD):
+                turns = turns + turn_q_steps(n + Q_TURN_AHEAD)
+            if live(n - MIX_LAG):
+                turns = turns + turn_share_steps(n - MIX_LAG)
+            per_gap = PACK if n == 0 else TURNS_PER_GAP
+            gaps = [turns[g * per_gap : (g + 1) * per_gap] for g in range(H * CHUNKS)]
+
+            for c in range(CHUNKS):
                 logit_pass(n, 1, c)
-                if c == PACK - 1:
+                if c == CHUNKS - 1:
                     scale_head1(n)
                 run(gaps[c])
             if live(n - 1):
                 scale_bias(n - 1)
             if n > 0 and live(n + 1):
                 copy_q(n + 1)
-            if live(m):
-                apply_gain(m, 0)
-            for c in range(PACK):
+            if live(n - MIX_LAG):
+                apply_gain(n - MIX_LAG, 0)
+            for c in range(CHUNKS):
                 logit_pass(n, 0, c)
-                run(gaps[PACK + c])
+                run(gaps[CHUNKS + c])
             if live(n - 1):
                 exponentials(n - 1)
             mix_logits(n)
             if live(n - OUT_LAG):
                 mix_values(n - OUT_LAG)
-            if live(m):
-                apply_gain(m, 1)
+            if live(n - MIX_LAG):
+                apply_gain(n - MIX_LAG, 1)
             if live(n - OUT_LAG):
                 store(n - OUT_LAG)
+
             if n == 0:
                 run(widen_v_steps(1, 0, nc.scalar))
                 weave_v(1, 0, nc.gpsimd)
             if n == 1:
-                last_v = widen_v_steps(1, 1, nc.scalar)
-                run(last_v[:2])
+                last_widen = widen_v_steps(1, 1, nc.scalar)
+                run(last_widen[: PACK // 2])
             if n == 2:
-                run(last_v[2:])
+                run(last_widen[PACK // 2 :])
 
         last = N_TILES - 1
+        spare_banks = (LOGIT_BANKS[1], LOGIT_BANKS[0])
 
         row_max(last)
         quantise_u(last - 4)
@@ -469,35 +477,38 @@ def tile_caittalkingheadsattention_t_kernel(tc, q, k, v_bytes, v_scale, mixl, mi
         scale_bias(last)
         run(turn_share_steps(last - 3))
         apply_gain(last - 3, 0)
-        weigh_head0(last - 1, 0, nc.vector)
-        weigh_head0(last - 1, 1, nc.vector)
+        share_head0(last - 1, 0, nc.vector)
+        share_head0(last - 1, 1, nc.vector)
         exponentials(last)
-        weigh_head1(last - 1, nc.scalar)
+        share_head1(last - 1, nc.scalar)
         mix_values(last - 4)
-        run(turn_share_steps(last - 2, ("q", "q")))
+        run(turn_share_steps(last - 2, Q_BANKS))
         apply_gain(last - 3, 1)
         invert_sums(last)
-        weigh_head1(last, nc.scalar)
+        share_head1(last, nc.scalar)
         store(last - 4)
+
         apply_gain(last - 2, 0)
-        weigh_head0(last, 0, nc.vector)
-        weigh_head0(last, 1, nc.vector)
+        share_head0(last, 0, nc.vector)
+        share_head0(last, 1, nc.vector)
         quantise_u(last - 3)
-        run(turn_share_steps(last - 1, ("l1", "l0")))
+        run(turn_share_steps(last - 1, spare_banks))
         mix_values(last - 3)
         store(last - 3)
+
         run(turn_share_steps(last))
         apply_gain(last - 2, 1)
         apply_gain(last - 1, 0)
         quantise_u(last - 2)
         mix_values(last - 2)
         store(last - 2)
+
         apply_gain(last - 1, 1)
         apply_gain(last, 0)
         quantise_u(last - 1)
-        mix_values(last - 1, ("q", "q"))
+        mix_values(last - 1, Q_BANKS)
         apply_gain(last, 1)
         quantise_u(last)
-        mix_values(last, ("l1", "l0"))
-        store(last - 1)
-        store(last)
+        mix_values(last, spare_banks)
+        store_by_head(last - 1)
+        store_by_head(last)

import math
from contextlib import ExitStack

import concourse.mybir as mybir
from concourse.masks import make_identity

B, H, T, S, E = 2, 2, 2048, 512, 512
FLOPS = 2 * 2 * B * H * T * S * E

F32 = mybir.dt.float32
BF16 = mybir.dt.bfloat16
U32 = mybir.dt.uint32
U8 = mybir.dt.uint8
FP8 = mybir.dt.float8_e4m3fn
FP8X4 = mybir.dt.float8_e4m3fn_x4
ALU = mybir.AluOpType
ACT = mybir.ActivationFunctionType
AXIS = mybir.AxisListType

P = 128
PACK = 4
CHUNKS = E // P
TILES_PER_BATCH = T // P
N_TILES = B * TILES_PER_BATCH

Q_LOAD_AHEAD = 4
Q_TURN_AHEAD = 2
SHARE_LAG = 2
MIX_LAG = 4
OUT_LAG = 5
TURNS_PER_GAP = 3

PIVOT_SHARE = 2.0**-40
PIVOT_FLOOR = 2.0**-100

Q_BANKS = ("q", "q")
LOGIT_BANKS = ("l0", "l1")
MIX_BANKS = ("m0", "m1")
OUT_BANKS = ("o0", "o1")


def tile_caittalkingheadsattention_t_kernel(tc, q, k, v_bytes, v_scale, mixl, mixw, gs, out):
    nc = tc.nc
    with ExitStack() as ctx:
        keep = ctx.enter_context(tc.tile_pool(name="keep", bufs=1))
        ring2 = ctx.enter_context(tc.tile_pool(name="ring2", bufs=2))
        ring3 = ctx.enter_context(tc.tile_pool(name="ring3", bufs=3))
        ring4 = ctx.enter_context(tc.tile_pool(name="ring4", bufs=4))
        psum = ctx.enter_context(tc.psum_pool(name="psum", bufs=1))
        ctx.enter_context(tc.manual_schedule())

        q_rows, q_bank, q_turned, l_bank, head1_logits, logits = {}, {}, {}, {}, {}, {}
        neg_max, exp_bias, expo, sums, inv_sum, shares = {}, {}, {}, {}, {}, {}
        mix_bank, u_wide, u_codes, u_scales, out_bank = {}, {}, {}, {}, {}
        k_rows, k_bank, k_turned = {}, {}, {}
        v_raw, v_planes, v_woven, v_codes, v_scales = {}, {}, {}, {}, {}

        def live(n):
            return 0 <= n < N_TILES

        def bank_tile(shape, dtype, name, tag):
            return psum.tile(shape, dtype, name=name, tag=tag, bufs=2 if tag in Q_BANKS else 1)

        def run(steps):
            for fn, args in steps:
                fn(*args)

        def copy(engine, dst, src):
            if engine is nc.scalar:
                nc.scalar.copy(out=dst, in_=src)
            else:
                engine.tensor_copy(out=dst, in_=src)

        def scalar_ops(dst, src, s1, op0, s2=None, op1=None):
            if op1 is None:
                nc.vector.tensor_scalar(out=dst, in0=src, scalar1=s1, scalar2=None, op0=op0)
            else:
                nc.vector.tensor_scalar(out=dst, in0=src, scalar1=s1, scalar2=s2, op0=op0, op1=op1)

        def scale_rows(engine, dst, src, factor):
            if engine is nc.scalar:
                nc.scalar.activation(out=dst, in_=src, func=ACT.Copy, scale=factor)
            else:
                scalar_ops(dst, src, factor, ALU.mult)


        def token_rows(dram, n):
            b, i = divmod(n, TILES_PER_BATCH)
            return dram[b, :, i * P : (i + 1) * P, :].rearrange("h p e -> p h e")

        def load_q(n):
            q_rows[n] = ring4.tile([P, H, E], BF16, name="q_rows")
            nc.sync.dma_start(out=q_rows[n][:], in_=token_rows(q, n))

        def load_k(b, h):
            k_rows[b, h] = keep.tile([P, PACK, E], BF16, name="k_rows_%d%d" % (b, h))
            nc.sync.dma_start(out=k_rows[b, h][:], in_=k[b, h].rearrange("(p t) e -> p t e", t=PACK))

        def load_v(b):
            v_raw[b] = keep.tile([P, H, PACK * E], U8, name="v_raw_%d" % b)
            nc.sync.dma_start(out=v_raw[b][:], in_=v_bytes[b].rearrange("h (p t) e -> p h (t e)", t=PACK))

        mixl_raw = keep.tile([P, H * H], BF16, name="mixl_raw")
        mixw_raw = keep.tile([P, H * H], BF16, name="mixw_raw")
        gs_raw = keep.tile([P, PACK], BF16, name="gs_raw")
        v_row_scale = keep.tile([P, PACK], F32, name="v_row_scale")

        nc.sync.dma_start(out=mixl_raw[:], in_=mixl.rearrange("h j -> (h j)").partition_broadcast(P))
        nc.sync.dma_start(out=mixw_raw[:], in_=mixw.rearrange("h j -> (h j)").partition_broadcast(P))
        load_q(0)
        load_k(0, 1)
        nc.sync.dma_start(out=gs_raw[:], in_=gs.rearrange("(p t) -> p t", t=PACK))
        nc.sync.dma_start(out=v_row_scale[:], in_=v_scale.rearrange("a b (p t) c -> p (a b t c)", t=PACK))
        load_v(0)
        load_q(1)
        load_k(0, 0)
        load_q(2)
        load_v(1)
        load_k(1, 0)
        load_q(3)
        load_k(1, 1)

        ident_bf16 = keep.tile([P, P], BF16, name="ident_bf16")
        ident_f32 = keep.tile([P, P], F32, name="ident_f32")
        make_identity(nc, ident_bf16[:])
        make_identity(nc, ident_f32[:])


        def column(name, width=1):
            return keep.tile([P, width], F32, name=name)

        def multiply(dst, a, b):
            nc.vector.tensor_tensor(out=dst, in0=a, in1=b, op=ALU.mult)

        def largest_magnitude(dst, src):
            nc.vector.tensor_reduce(out=dst, in_=src, axis=AXIS.X, op=ALU.max, apply_absolute_value=True)

        def invert(dst, src):
            nc.vector.reciprocal(out=dst, in_=src)

        def pivot_steps(name, matrix, pivots):
            top, floor = column(name + "_top"), column(name + "_floor")
            twice, sign = column(name + "_twice", H), column(name + "_sign", H)
            bare, size, inverse = column(name + "_bare", H), column(name + "_size", H), column(name + "_inverse", H)
            steps = [
                (largest_magnitude, (top[:], matrix)),
                (scalar_ops, (twice[:], pivots, 0.0, ALU.is_ge, 2.0, ALU.mult)),
                (scalar_ops, (floor[:], top[:], PIVOT_SHARE, ALU.mult, PIVOT_FLOOR, ALU.max)),
                (scalar_ops, (sign[:], twice[:], 1.0, ALU.subtract)),
                (multiply, (bare[:], pivots, sign[:])),
                (scalar_ops, (size[:], bare[:], floor[:], ALU.max)),
                (invert, (inverse[:], size[:])),
            ]
            return steps, sign, size, inverse

        l_steps, l_sign, l_size, l_inverse = pivot_steps("l", mixl_raw[:], mixl_raw[:, 0:4:3])
        head1_scale, logit_scale, l_ratio = column("head1_scale"), column("logit_scale"), column("l_ratio", H)
        l_steps = l_steps + [
            (scalar_ops, (logit_scale[:], l_size[:, 0:1], 1.0 / math.sqrt(E), ALU.mult)),
            (scalar_ops, (head1_scale[:], l_size[:, 1:2], l_sign[:, 1:2], ALU.mult, l_inverse[:, 0:1], ALU.mult)),
            (scalar_ops, (l_ratio[:, 0:1], mixl_raw[:, 2:3], l_sign[:, 1:2], ALU.mult, l_inverse[:, 1:2], ALU.mult)),
            (scalar_ops, (l_ratio[:, 1:2], mixl_raw[:, 1:2], l_sign[:, 0:1], ALU.mult, l_inverse[:, 0:1], ALU.mult)),
        ]

        w_steps, w_sign, w_size, w_inverse = pivot_steps("w", mixw_raw[:], mixw_raw[:, 2:4])
        w_pivot, w_signed, w_ratio = column("w_pivot", H), column("w_signed", H), column("w_ratio", H)
        key_gain = keep.tile([P, H, P, PACK], F32, name="key_gain")
        gs_spread = gs_raw[:].rearrange("p (o t) -> p o t", o=1).to_broadcast([P, P, PACK])
        w_steps = w_steps + [
            (multiply, (w_pivot[:], w_size[:], w_sign[:])),
            (multiply, (w_signed[:], mixw_raw[:, 0:2], w_sign[:])),
            (scalar_ops, (key_gain[:, 0, :, :], gs_spread, w_pivot[:, 0:1], ALU.mult, math.sqrt(S), ALU.mult)),
            (multiply, (w_ratio[:], w_signed[:], w_inverse[:])),
            (scalar_ops, (key_gain[:, 1, :, :], gs_spread, w_pivot[:, 1:2], ALU.mult, math.sqrt(S), ALU.mult)),
        ]


        def turn_k(b, h, c, t, engine):
            if t == 0:
                k_bank[b, h, c] = bank_tile([P, S], BF16, "k_bank", (MIX_BANKS + OUT_BANKS)[c])
            half, parity = divmod(c, 2)
            e0 = 2 * P * half + parity
            nc.tensor.transpose(
                k_bank[b, h, c][:, t * P : (t + 1) * P], k_rows[b, h][:, t, e0 : e0 + 2 * P - 1 : 2], ident_bf16[:]
            )
            if t == PACK - 1:
                k_turned[b, h, c] = keep.tile([P, S], BF16, name="k_turned_%d%d%d" % (b, h, c))
                if h == 1:
                    copy(engine, k_turned[b, h, c][:], k_bank[b, h, c][:])
                else:
                    scale_rows(engine, k_turned[b, h, c][:], k_bank[b, h, c][:], l_sign[:, 0:1])

        def turn_k_steps(b, h, engine):
            return [(turn_k, (b, h, c, t, engine)) for c in range(CHUNKS) for t in range(PACK)]

        def turn_q(n, group):
            if group == 0:
                q_bank[n] = bank_tile([P, 2 * H, P], F32, "q_bank", Q_BANKS[0])
            words = q_rows[n][:].rearrange("p h e -> p (h e)").bitcast(F32)
            nc.tensor.transpose(q_bank[n][:, group, :], words[:, group * P : (group + 1) * P], ident_f32[:])

        def turn_q_steps(n):
            return [(turn_q, (n, group)) for group in range(2 * H)]

        def copy_q(n):
            q_turned[n] = ring2.tile([P, 2 * H * P], F32, name="q_turned")
            nc.scalar.copy(out=q_turned[n][:], in_=q_bank[n][:].rearrange("p g n -> p (g n)"))


        def logit_pass(n, h, c):
            if c == 0:
                l_bank[n, h] = bank_tile([P, S], F32, "l_bank", LOGIT_BANKS[h])
            half, parity = divmod(c, 2)
            col0 = (2 * h + half) * 2 * P + parity
            pairs = q_turned[n][:].bitcast(BF16)
            nc.tensor.matmul(
                l_bank[n, h][:],
                lhsT=pairs[:, col0 : col0 + 2 * P - 1 : 2],
                rhs=k_turned[n // TILES_PER_BATCH, h, c][:],
                start=(c == 0),
                stop=(c == CHUNKS - 1),
            )

        def scale_head1(n):
            head1_logits[n] = ring2.tile([P, S], F32, name="head1_logits")
            scale_rows(nc.scalar, head1_logits[n][:], l_bank[n, 1][:], head1_scale[:])

        def mix_logits(n):
            logits[n] = ring2.tile([P, H, S], F32, name="logits")
            terms = [l_bank[n, 0][:], head1_logits[n][:]]
            for j in range(H):
                nc.vector.scalar_tensor_tensor(
                    out=logits[n][:, j, :],
                    in0=terms[1 - j],
                    scalar=l_ratio[:, j : j + 1],
                    in1=terms[j],
                    op0=ALU.mult,
                    op1=ALU.add,
                )

        def row_max(n):
            neg_max[n] = ring3.tile([P, H], F32, name="neg_max")
            nc.vector.tensor_reduce(out=neg_max[n][:], in_=logits[n][:], axis=AXIS.X, op=ALU.max, negate=True)

        def scale_bias(n):
            exp_bias[n] = ring3.tile([P, H], F32, name="exp_bias")
            scale_rows(nc.scalar, exp_bias[n][:], neg_max[n][:], logit_scale[:])

        def exponentials(n):
            expo[n] = ring2.tile([P, H, S], F32, name="expo")
            sums[n] = ring3.tile([P, H], F32, name="sums")
            for h in range(H):
                nc.scalar.activation(
                    out=expo[n][:, h, :],
                    in_=logits[n][:, h, :],
                    func=ACT.Exp,
                    bias=exp_bias[n][:, h : h + 1],
                    scale=logit_scale[:],
                    accum_out=sums[n][:, h : h + 1],
                )

        def invert_sums(n):
            inv_sum[n] = ring3.tile([P, H], F32, name="inv_sum")
            invert(inv_sum[n][:], sums[n][:])

        def share_head0(n, j, engine):
            shares[n, j, 0] = ring3.tile([P, S], F32, name="share_%d" % j)
            engine.tensor_scalar(
                out=shares[n, j, 0][:],
                in0=expo[n][:, 0, :],
                scalar1=inv_sum[n][:, 0:1],
                scalar2=w_ratio[:, j : j + 1],
                op0=ALU.mult,
                op1=ALU.mult,
            )

        def share_head1(n, engine):
            shares[n, 0, 1] = ring3.tile([P, S], F32, name="share_both")
            shares[n, 1, 1] = shares[n, 0, 1]
            if engine is nc.scalar:
                scale_rows(nc.scalar, shares[n, 0, 1][:], expo[n][:, 1, :], inv_sum[n][:, 1:2])
            else:
                nc.gpsimd.tensor_scalar(
                    out=shares[n, 0, 1][:],
                    in0=expo[n][:, 1, :],
                    scalar1=inv_sum[n][:, 1:2],
                    scalar2=0.0,
                    op0=ALU.mult,
                    op1=ALU.add,
                )

        def turn_share(n, j, t, h, tag):
            if t == 0 and h == 0:
                mix_bank[n, j] = bank_tile([P, PACK, P], F32, "mix_bank", tag)
            nc.tensor.matmul(
                mix_bank[n, j][:, t, :],
                lhsT=shares[n, j, h][:, t * P : (t + 1) * P],
                rhs=ident_f32[:],
                is_transpose=True,
                start=(h == 0),
                stop=(h == H - 1),
            )

        def turn_share_steps(n, tags=MIX_BANKS):
            return [(turn_share, (n, j, t, h, tags[j])) for j in range(H) for t in range(PACK) for h in range(H)]

        def apply_gain(n, j):
            if j == 0:
                u_wide[n] = ring2.tile([P, H, P, PACK], BF16, name="u_wide", align_bytes=64)
            nc.vector.tensor_tensor(
                out=u_wide[n][:, j, :, :],
                in0=mix_bank[n, j][:].rearrange("p t n -> p n t"),
                in1=key_gain[:, j, :, :],
                op=ALU.mult,
            )

        def quantise_u(n):
            u_codes[n] = ring2.tile([P, H * P], U32, name="u_codes", align_bytes=64)
            u_scales[n] = ring2.tile([P, H * P], U8, name="u_scales", align_bytes=64)
            nc.vector.quantize_mx(
                out=u_codes[n][:].bitcast(FP8X4),
                scales=u_scales[n][:],
                in_=u_wide[n][:].rearrange("p j n t -> p (j n t)"),
            )

        def mix_values(n, tags=OUT_BANKS):
            b = n // TILES_PER_BATCH
            for j in range(H):
                out_bank[n, j] = bank_tile([P, E], F32, "out_bank", tags[j])
                nc.tensor.matmul_mx(
                    out=out_bank[n, j][:],
                    lhsT=u_codes[n][:, j * P : (j + 1) * P].bitcast(FP8X4),
                    lhsT_scale=u_scales[n][:, j * P : (j + 1) * P],
                    rhs=v_codes[b, j][:].bitcast(FP8X4),
                    rhs_scale=v_scales[b, j][:],
                    start=True,
                    stop=True,
                )

        def store(n):
            result = ring3.tile([P, H, E], F32, name="result")
            for j in range(H):
                nc.scalar.copy(out=result[:, j, :], in_=out_bank[n, j][:])
            nc.sync.dma_start(out=token_rows(out, n), in_=result[:])

        def store_by_head(n):
            result = ring3.tile([P, H, E], F32, name="result")
            for j, engine in enumerate([nc.scalar, nc.vector]):
                copy(engine, result[:, j, :], out_bank[n, j][:])
                nc.sync.dma_start(out=token_rows(out, n)[:, j, :], in_=result[:, j, :])


        def widen_v_steps(b, j, engine):
            v_planes[b, j] = ring2.tile([P, PACK, E], BF16, name="v_planes")
            return [
                (
                    scale_rows,
                    (
                        engine,
                        v_planes[b, j][:, t, :],
                        v_raw[b][:, j, t * E : (t + 1) * E].bitcast(FP8),
                        v_row_scale[:, t : t + 1],
                    ),
                )
                for t in range(PACK)
            ]

        def weave_v(b, j, engine):
            v_woven[b, j] = ring2.tile([P, E, PACK], BF16, name="v_woven", align_bytes=64)
            planes = v_planes[b, j][:].rearrange("p t e -> p e t")
            if engine is nc.gpsimd:
                nc.gpsimd.tensor_scalar(
                    out=v_woven[b, j][:], in0=planes, scalar1=1.0, scalar2=0.0, op0=ALU.mult, op1=ALU.add
                )
            else:
                nc.vector.tensor_copy(out=v_woven[b, j][:], in_=planes)

        def quantise_v(b, j):
            v_codes[b, j] = keep.tile([P, E], U32, name="v_codes_%d%d" % (b, j), align_bytes=64)
            v_scales[b, j] = keep.tile([P, E], U8, name="v_scales_%d%d" % (b, j), align_bytes=64)
            nc.vector.quantize_mx(
                out=v_codes[b, j][:].bitcast(FP8X4),
                scales=v_scales[b, j][:],
                in_=v_woven[b, j][:].rearrange("p e t -> p (e t)"),
            )

        for pair in zip(l_steps, w_steps):
            run(pair)
        run(w_steps[len(l_steps) :])
        run(turn_q_steps(0))
        copy_q(0)
        first_k = turn_k_steps(0, 1, nc.scalar) + turn_k_steps(0, 0, nc.scalar)
        run(first_k[: 2 * PACK])
        run(turn_q_steps(1))
        for j in range(H):
            run(widen_v_steps(0, j, nc.vector))
        for j in range(H):
            weave_v(0, j, nc.vector)
        for j in range(H):
            quantise_v(0, j)

        k_jobs = {1: (1, 0, nc.vector), 3: (1, 1, nc.scalar)}

        for n in range(N_TILES):
            if live(n + Q_LOAD_AHEAD):
                load_q(n + Q_LOAD_AHEAD)
            if live(n - 1):
                row_max(n - 1)
            if n == 0:
                copy_q(1)

            if live(n - OUT_LAG):
                quantise_u(n - OUT_LAG)
            if n == 2:
                quantise_v(1, 0)
            if n == 3:
                weave_v(1, 1, nc.vector)
            if n == 4:
                quantise_v(1, 1)
            if live(n - SHARE_LAG):
                invert_sums(n - SHARE_LAG)
                share_head0(n - SHARE_LAG, 0, nc.gpsimd)
                share_head1(n - SHARE_LAG, nc.gpsimd)
                share_head0(n - SHARE_LAG, 1, nc.gpsimd)

            turns = []
            if n == 0:
                turns = first_k[2 * PACK :]
            if n in k_jobs:
                turns = turn_k_steps(*k_jobs[n])
            if live(n + Q_TURN_AHEAD):
                turns = turns + turn_q_steps(n + Q_TURN_AHEAD)
            if live(n - MIX_LAG):
                turns = turns + turn_share_steps(n - MIX_LAG)
            per_gap = PACK if n == 0 else TURNS_PER_GAP
            gaps = [turns[g * per_gap : (g + 1) * per_gap] for g in range(H * CHUNKS)]

            for c in range(CHUNKS):
                logit_pass(n, 1, c)
                if c == CHUNKS - 1:
                    scale_head1(n)
                run(gaps[c])
            if live(n - 1):
                scale_bias(n - 1)
            if n > 0 and live(n + 1):
                copy_q(n + 1)
            if live(n - MIX_LAG):
                apply_gain(n - MIX_LAG, 0)
            for c in range(CHUNKS):
                logit_pass(n, 0, c)
                run(gaps[CHUNKS + c])
            if live(n - 1):
                exponentials(n - 1)
            mix_logits(n)
            if live(n - OUT_LAG):
                mix_values(n - OUT_LAG)
            if live(n - MIX_LAG):
                apply_gain(n - MIX_LAG, 1)
            if live(n - OUT_LAG):
                store(n - OUT_LAG)

            if n == 0:
                run(widen_v_steps(1, 0, nc.scalar))
                weave_v(1, 0, nc.gpsimd)
            if n == 1:
                last_widen = widen_v_steps(1, 1, nc.scalar)
                run(last_widen[: PACK // 2])
            if n == 2:
                run(last_widen[PACK // 2 :])

        last = N_TILES - 1
        spare_banks = (LOGIT_BANKS[1], LOGIT_BANKS[0])

        row_max(last)
        quantise_u(last - 4)
        invert_sums(last - 1)
        scale_bias(last)
        run(turn_share_steps(last - 3))
        apply_gain(last - 3, 0)
        share_head0(last - 1, 0, nc.vector)
        share_head0(last - 1, 1, nc.vector)
        exponentials(last)
        share_head1(last - 1, nc.scalar)
        mix_values(last - 4)
        run(turn_share_steps(last - 2, Q_BANKS))
        apply_gain(last - 3, 1)
        invert_sums(last)
        share_head1(last, nc.scalar)
        store(last - 4)

        apply_gain(last - 2, 0)
        share_head0(last, 0, nc.vector)
        share_head0(last, 1, nc.vector)
        quantise_u(last - 3)
        run(turn_share_steps(last - 1, spare_banks))
        mix_values(last - 3)
        store(last - 3)

        run(turn_share_steps(last))
        apply_gain(last - 2, 1)
        apply_gain(last - 1, 0)
        quantise_u(last - 2)
        mix_values(last - 2)
        store(last - 2)

        apply_gain(last - 1, 1)
        apply_gain(last, 0)
        quantise_u(last - 1)
        mix_values(last - 1, Q_BANKS)
        apply_gain(last, 1)
        quantise_u(last)
        mix_values(last, spare_banks)
        store_by_head(last - 1)
        store_by_head(last)
